import numpy as np, ml_dtypes
CORES = [3,11,19,27,35,43,51,59]
N = 8
import mx_ref
BF = ml_dtypes.bfloat16
def gcols(t, e):
    v = np.concatenate([t.reshape(8, 16, -1, 4), np.zeros((8, 16, 1, 4), BF)], axis=2)
    return np.ascontiguousarray(np.stack([v[g][:, e[g]] for g in range(8)])).reshape(128, -1)
def tile(rs):
    return np.stack(rs, axis=2).reshape(128, -1).astype(BF)
def pick(q, e):
    c = np.concatenate([q[0].reshape(128, -1, 4), np.zeros((128, 1, 4), np.uint8)], axis=1); s = np.concatenate([q[1], np.ones((16, 1), np.uint8)], axis=1)
    return (np.ascontiguousarray(c[:, e].reshape(128, -1)), np.ascontiguousarray(s[:, e]))
def join(*qs):
    return (np.concatenate([q[0] for q in qs], axis=1), np.concatenate([q[1] for q in qs], axis=1))
def put(q, e, v):
    c, s = q[0].reshape(128, -1, 4).copy(), q[1].copy(); c[:, e] = v[0].reshape(128, -1, 4); s[:, e] = v[1]
    return (c.reshape(128, -1), s)
def pk(c, s):
    return (np.ascontiguousarray(c), mx_ref.live(s))
def emit(q):
    return q[0], q[1]
def packed(v, rng):
    q = [mx_ref.quantize(np.ascontiguousarray(v[r])) for r in range(N)]
    return np.stack([a for a, b in q]), np.stack([mx_ref.plane(b, rng) for a, b in q])
def values_of_codes():
    e, c = np.zeros((128, 128, 4), np.float32), np.zeros((128, 2, 4), np.uint8)
    e[np.arange(128), np.arange(128), 0] = 1
    c[:127, :, 0] = np.arange(256).reshape(2, 128).T[:127]
    return mx_ref.matmul(mx_ref.quantize(e.reshape(128, 512).astype(BF)), (c.reshape(128, 8), np.full((16, 2), 127, np.uint8))).T.reshape(-1).astype(np.float64)
CODE_VALUE, SCALE_VALUE = values_of_codes(), 2.0 ** (np.arange(256) - 127.0)
def decode(q):
    return (CODE_VALUE[q[0]].reshape(16, 8, -1, 4) * SCALE_VALUE[q[1]][:, None, :, None] + 0.0).reshape(128, -1).astype(np.float32)
def f(rng, *shape):
    return mx_ref.flush((rng.standard_normal(shape, dtype=np.float32) * np.exp2(rng.integers(-2, 3, shape[:-1] + (1,)))).astype(BF))
def wide(rng, *shape, cols=0):
    v = rng.standard_normal(shape, dtype=np.float32) * np.exp2(rng.integers(-12, 13, shape)).astype(np.float32)
    if cols: v *= np.repeat(np.exp2(rng.integers(-cols, cols + 1, shape[:-2] + (1, shape[-1] // 4))) * (rng.random(shape[:-2] + (1, shape[-1] // 4)) > 0.0625), 4, axis=-1).astype(np.float32)
    return mx_ref.flush(v.astype(BF))
C, P, R = 320, 80, 2
def big(v):
    v = v.astype(np.float32)
    v[np.abs(v) < np.float32(2.0 ** -16)] = 0
    return v.astype(BF)
def numbers_of(rng):
    return {"x": big(f(rng, N, 128, 4 * C)), "u": np.array(f(rng, N, 128, 512)), "v": np.array(f(rng, N, 128, 512))}
def layers(rng):
    return big(f(rng, N, 128, 2048)).reshape(N, 8, 16, 4, 8, 16, 4)
def weights(rng, w):
    c, p = packed(np.ascontiguousarray(w).reshape(N, 128, 2048), rng)
    return {"wc": c, "ws": p}
def setup_inputs(rng):
    return {**numbers_of(rng), **weights(rng, layers(rng))}
def setup_inputs_ties(rng):
    d = numbers_of(rng)
    e = rng.permutation(N)
    x = d["x"].reshape(N, 8, 16, C, 4)
    for r in range(N):
        k = rng.permutation(C) % 3
        if r == e[0]: k = np.zeros(C, int)
        elif r in e[2::2]: k = rng.permutation(3)[np.arange(C) % 3]
        a = x[r][:, :8, :3].copy()
        a[:, :, 2] = 0
        x[r][:, :8] = a[:, :, k]
    x[e[1]] = 0
    u = d["u"].reshape(N, 8, 16, 128, 4)
    for i in range(5): u[:, :, 8:, i::16] = 0
    w = layers(rng)
    w[:, :, :, :, :, :8] = 0
    return {"x": x.reshape(N, 128, 4 * C), "u": u.reshape(N, 128, 512), "v": d["v"], **weights(rng, w)}
def setup_inputs_near(rng):
    d = numbers_of(rng)
    x = d["x"].astype(np.float32).reshape(N, 8, 16, C, 4)
    x[:, :, :9] = 0
    u = d["u"].reshape(N, 128, 128, 4)
    for i in range(5): u[:, :, i::16] = 0
    o = rng.permutation(N) % 4
    for r in range(N):
        k = 2.0 ** -30 if o[r] else 1.0
        c = rng.integers(0, 2, (8, 1)) * 2.0 - 1.0
        s = rng.integers(-1, 2, (8, C, 4))
        if o[r] < 2:
            n = rng.integers(0, 16, (8, C))
            x[r, :, 0] = ((n[:, :, None] >> np.arange(4)) & 1) * np.exp2(np.arange(4) - 23.0)
            x[r, :, 1, :, 0] = 2.0 ** -10
            x[r, :, 2] = s * 2.0 ** -10
            x[r, :, 8, :, 0] = c
        else:
            x[r, :, 0, :, 0] = c * rng.integers(1, 16, (8, C)) * 2.0 ** -29
            x[r, :, 2] = s * 2.0 ** -29
        for g in rng.permutation(8)[:4]: x[r, g, 8 if o[r] < 2 else 0, rng.integers(C), 0] = 2.0 ** 29 * (rng.integers(0, 2) * 2.0 - 1.0)
        for h in range(0, 128, 16):
            u[r, h, h + 4] = k
            u[r, h + 1, h + 4, 0] = k
            u[r, h + 8, h + 4, 0] = k
            for i in range(4): u[r, h + 2, h + i, i] = k
    w = layers(rng)
    w[:, :, :9] = 0
    w[:, :, :, :, :, :9] = 0
    return {"x": x.reshape(N, 128, 4 * C).astype(BF), "u": u.reshape(N, 128, 512), "v": d["v"], **weights(rng, w)}
def setup_inputs_skew(rng):
    d = numbers_of(rng)
    x = d["x"].astype(np.float32).reshape(N, 8, 16, C, 4)
    t = (1 + (2 * rng.integers(0, 64, (N, 8, 8, C // 2, 4)) + 1) / 128) * np.exp2(-rng.integers(8, 15, (N, 8, 8, C // 2, 4)).astype(float)) * (rng.integers(0, 2, (N, 8, 8, C // 2, 4)) * 2.0 - 1.0)
    t[:, :, 3, :, 1] = 1.96875
    x[:, :, 8:, ::2] = t * np.exp2(rng.integers(-2, 3, (N, 8, 1, C // 2, 1)).astype(float))
    u = d["u"].reshape(N, 128, 128, 4)
    for i in range(5): u[:, :, i::16] = 0
    for h in range(0, 128, 16):
        for b in range(12): u[:, h + b // 4, h + 4, b % 4] = 2.0 ** b
        for i in range(4): u[:, h + 3, h + i, i] = 1
    n = -(-C // 7)
    n2 = n - (-(C - n) // 5)
    n3 = n2 - (-(C - n2) // 3)
    down = C - 1 - np.arange(C)
    for r in range(N):
        for j, g in enumerate(rng.permutation(8)):
            a = np.append(rng.permutation(np.delete(np.arange(4), j % 4)), j % 4)
            two = np.zeros((C, 4), int)
            if j < 6:
                two[:n, a[0]] = 1
                two[n:n2, a[1]] = 1
            if j < 4: two[n2:n3, a[2]] = 1
            if j >= 6: two[-(-2 * C // 5):] = 1
            o = rng.permutation(C)
            x[r, g][:3, o] = (down[None, :, None] >> (4 * np.arange(3)[:, None, None] + np.arange(4))) & 1
            x[r, g][3, o] = np.where(two > 0, 1, -rng.integers(0, 2, (C, 4)))
    w = layers(rng)
    w[:, :, :, :, :, :4] = 0
    return {"x": x.reshape(N, 128, 4 * C).astype(BF), "u": u.reshape(N, 128, 512), "v": d["v"], **weights(rng, w)}
def setup_inputs_huge(rng):
    d = numbers_of(rng)
    o = rng.permutation(N)
    h = rng.permutation(8)
    x = -0.95 - 0.05 * rng.random((N, 8, 16, C, 4))
    x[:, h[4:]] = (0.75 + 0.1 * rng.random((N, 4, 16, C, 4))) * rng.choice([-1.0, 1.0], (N, 4, 1, C, 1))
    u = d["u"].reshape(N, 128, 128, 4)
    for i in range(5): u[:, :, i::16] = 0
    for r in range(N):
        if o[r] < N // 2: x[r] = (0.8 + 0.1 * rng.random((8, 16, C, 4))) * rng.choice([-1.0, 1.0], (1, 1, C, 1))
        for g in range(8):
            for i in range(5):
                a, n = 16 * int(rng.choice(h[4:])), 16
                if i == 4 and o[r] < N // 2: a, n = 0, 128
                u[r, a:a + n, 16 * g + i] = (2.0 ** 30 * (1 - 0.05 * rng.random((n, 4))) * rng.choice([-1.0, 1.0])).astype(np.float32).astype(BF)
    w = np.zeros((N, 128, 4, 128, 4), np.float32)
    i = np.arange(128)
    for b in range(4): w[:, i, b, i, b] = -1
    return {"x": (2.0 ** 30 * x).astype(np.float32).reshape(N, 128, 4 * C).astype(BF), "u": u.reshape(N, 128, 512), "v": d["v"], **weights(rng, w.astype(BF))}
def setup_inputs_spread(rng):
    d = setup_inputs(rng)
    d["x"] = big(wide(rng, N, 128, 4 * C, cols=6))
    return d
def check_inputs(d):
    b = []
    for k in ("x", "u", "v"):
        a = np.abs(d[k].astype(np.float32))
        if not (np.isfinite(a).all() and ((a == 0) | (a >= 2.0 ** -30) & (a <= 2.0 ** 30)).all()): b.append("a value of " + k)
    none, least, most = [emit(mx_ref.quantize(np.full((128, 16), k, np.float32).astype(BF)))[1][0, 0] for k in (0.0, 2.0 ** -30, 2.0 ** 30)]
    for r in range(N):
        if ((d["wc"][r] == 0x7F) | (d["wc"][r] == 0xFF)).any(): b.append("wc: a code that is no number")
        s = mx_ref.live(d["ws"][r])
        if ((s != none) & ((s < least) | (s > most))).any(): b.append("ws: a scale out of range")
    return b
def divide(sums):
    g = np.arange(8)
    first, end = np.zeros((4, 8), np.int64), np.full((4, 8), C)
    a, left = np.zeros(8, np.int64), np.ones((4, 8), bool)
    for m in (4, 3, 2):
        worth = sums - np.stack([sums[k, g, a] for k in range(4)])[:, :, None]
        e = np.sum(m * worth < worth[:, :, -1:], axis=2)
        e[~left] = C + 1
        k = np.argmin(e, axis=0)
        first[k, g] = a
        a = e[k, g]
        end[k, g] = a
        left[k, g] = False
    first[np.argmax(left, axis=0), g] = a
    return first, end
def reference(x, u, v, wc, ws):
    qu = [mx_ref.quantize(u[r]) for r in range(N)]
    lay = [pk(wc[r], ws[r]) for r in range(N)]
    now = [x[r] for r in range(N)]
    of = [np.arange(k * P, k * P + P) for k in range(4)]
    slot_of = np.zeros((N, 8, C), np.int64)
    for t in range(R):
        sent, best, made = [], [], []
        slot_of[:] = -1
        for r in range(N):
            s = mx_ref.matmul(qu[r], mx_ref.quantize(now[r])) + np.float32(0.0)
            o = np.argsort(-s[4::16], axis=1, kind="stable")
            worth = np.stack([1 + (np.take_along_axis(s[k::16], o, axis=1) > 0) for k in range(4)])
            first, end = divide(np.concatenate([np.zeros((4, 8, 1), np.int64), np.cumsum(worth, axis=2)], axis=2))
            slots = []
            for k in range(4):
                i = first[k][:, None] + np.arange(P)
                slots.append(np.where(i < end[k][:, None], np.take_along_axis(o, np.minimum(i, C - 1), axis=1), -1))
            slots = np.concatenate(slots, axis=1)
            for g in range(8):
                j = np.nonzero(slots[g] >= 0)[0]
                slot_of[r, g, slots[g, j]] = j
            sent.append(mx_ref.quantize(gcols(now[r], slots)))
            best.append(gcols(now[r], o[:, :P]))
        for r in range(N):
            came = decode(join(*[pick(sent[(r - k) % N], of[k]) for k in range(4)]))
            z = mx_ref.quantize(((came + np.tile(best[r].astype(np.float32), (1, 4))) * np.float32(0.5)).astype(BF))
            made.append(mx_ref.quantize(tile([mx_ref.matmul(pick(lay[r], np.arange(128 * b, 128 * b + 128)), z) * np.float32(0.03125) for b in range(4)])))
        for r in range(N):
            back = decode(join(*[pick(made[(r + k) % N], of[k]) for k in range(4)])).astype(BF)
            now[r] = (now[r].astype(np.float32) + gcols(back, slot_of[r]).astype(np.float32)).astype(BF)
    y, sl = np.zeros((N, 128, C), np.float32), np.zeros((N, 8, C), np.float32)
    oc, osc = np.zeros((N, 128, 4 * C), np.uint8), np.zeros((N, 16, C), np.uint8)
    for r in range(N):
        q = mx_ref.quantize(now[r])
        y[r] = mx_ref.matmul(mx_ref.quantize(v[r]), q)
        sl[r] = slot_of[r]
        oc[r], osc[r] = emit(q)
    return {"y": y, "sl": sl, "oc": oc, "osc": osc}

@@ -1,0 +1,527 @@
+from concourse.bass import DstId, RemoteDMATransfer
+from concourse.mybir import dt, AluOpType as OP, AxisListType, ActivationFunctionType as AF
+
+F32, BF, I32, U16, U8, F8 = "float32", "bfloat16", "int32", "uint16", "uint8", "float8_e4m3fn_x4"
+NR = 2
+UNIT = 2.0 ** 20
+NEG = 2.0 ** 97
+B16 = 1024.0
+B4 = 2.0 ** 21
+ACT_COLS = [0, 0, 128, 192, 256]
+
+
+def _scratch():
+    s = {}
+
+    def sb(dtype, **kw):
+        for n in kw:
+            s[n] = ("sbuf", [128, kw[n]], dtype)
+
+    def code(n, w):
+        s[n] = ("sbuf", [128, w], F8)
+        s[n + "s"] = ("sbuf", [128, w], U8)
+    sb(BF, x0=1296, x1=1296, x2=1296, ut=512, vt=512, eg=512, one=512, half=512, id4=512, un=2048, btile=1472, eh=960,
+       z0=512, h0=512, z1=960, h1=960, bk=1296, junk=320)
+    for b in range(5):
+        sb(BF, **{"ct%d" % b: 1280})
+    for n, w in (("qu", 128), ("qur", 128), ("qv", 128), ("wq", 512), ("qx", 320), ("qeg", 128), ("qun", 512),
+                 ("qbo", 128), ("qzo", 128), ("qho", 128), ("qz1", 240), ("qc0", 320), ("qc1", 320), ("qc2", 320)):
+        code(n, w)
+    for r in range(NR):
+        for n in ("qb", "qh", "came", "back"):
+            code("%s%d" % (n, r), 240)
+    sb(F32, i16=320, i4=400, ij=336, mm=320, d0=320, rs=320, k16=320, k4=400, ta=400, tb=400, d1=320,
+       st=320, eq=320, rc=336, rcb=20, pc=8, v4=320, wrow=336, cw=328, on=320, rx=320, rk=20, acc=8, gg=48, ee=48,
+       iw=336, lm=16, sm=128, tab=16, te=48, sc=20, pl=80, wsl=400, ox=400, tf=160, rks=80, kc=80, sl1=400, sl2=80)
+    sb(I32, pi=8, xi=64, oi=200, po=20)
+    sb(U16, ul=8, xl=4, l80=10, rk16=20, e16=8, off16=20, off4=100, po16=100)
+    for b in range(8):
+        s["p%d" % b] = ("psum", [128, 512], F32)
+    return s
+
+
+SCRATCH = _scratch()
+SEMAPHORES = (["sV", "sA", "sP", "sG", "gd", "ls", "dx", "du", "dw", "dv", "out"]
+              + ["ab%d" % r for r in range(NR)] + ["ah%d" % r for r in range(NR)])
+
+
+def tracker(g, T):
+    eng = {"V": g.vector, "A": g.scalar, "P": g.tensor, "G": g, "S": g.sync}
+    sem = {"V": "sV", "A": "sA", "P": "sP", "G": "sG"}
+    count = {q: 0 for q in sem}
+    known = {q: {} for q in eng}
+    known["far"] = {}
+    clock = {}
+    log = {}
+
+    def split(k):
+        a = k.split("/")
+        return a[0], (a[1] if len(a) > 1 else None)
+
+    def need(q, reads, writes, acc):
+        out = {}
+        for keys, w in ((reads, False), (writes, True)):
+            for k in keys:
+                n, s = split(k)
+                psum = n[0] == "p" and n[1:].isdigit()
+                for (s2, q2, tok, w2) in log.get(n, []):
+                    if not psum and s is not None and s2 is not None and s != s2:
+                        continue
+                    dma = tok[0] not in ("sV", "sA", "sP", "sG")
+                    if q2 == q and not dma:
+                        if (not w2 and not w) or (acc and w):
+                            continue
+                    elif not w and not w2 and not psum:
+                        continue
+                    out[tok[0]] = max(out.get(tok[0], 0), tok[1])
+        return out
+
+    def wait(q, toks):
+        for s in sorted(toks):
+            if known[q].get(s, 0) < toks[s]:
+                eng[q].wait_ge(T.sem[s], toks[s])
+                for (s2, v2) in clock.get((s, toks[s]), {}).items():
+                    known[q][s2] = max(known[q].get(s2, 0), v2)
+                known[q][s] = max(known[q].get(s, 0), toks[s])
+
+    def note(q, tok, reads, writes):
+        c = dict(known[q])
+        c[tok[0]] = max(c.get(tok[0], 0), tok[1])
+        if tok in clock:
+            for s2 in clock[tok]:
+                c[s2] = max(c.get(s2, 0), clock[tok][s2])
+        clock[tok] = c
+        for k in writes:
+            n, s = split(k)
+            log[n] = [e for e in log.get(n, []) if not (s is None or e[0] == s)] + [(s, q, tok, True)]
+        for k in reads:
+            n, s = split(k)
+            log[n] = [e for e in log.get(n, []) if not (not e[3] and e[1] == q and e[0] == s)] + [(s, q, tok, False)]
+
+    def tr(q, fn, reads, writes, acc=False):
+        wait(q, need(q, reads, writes, acc))
+        count[q] += 1
+        fn(eng[q]).then_inc(T.sem[sem[q]], 1)
+        note(q, (sem[q], count[q]), reads, writes)
+
+    def dma(q, fn, tok, reads, writes):
+        wait(q, need(q, reads, writes, False))
+        fn(eng[q]).then_inc(T.sem[tok[0]], 16)
+        note(q, tok, reads, writes)
+
+    def remote(fn, tok, reads):
+        wait("G", need("G", reads, [], False))
+        fn(g)
+        note("G", tok, reads, [])
+
+    def arrive(tok, writes):
+        note("far", tok, [], writes)
+    return tr, dma, remote, arrive
+
+
+def rank_program(g, core, T, topo):
+    rank = T.rank_of(core)
+    if rank is None:
+        return
+    N = len(T.cores)
+    tr, dma, remote, arrive = tracker(g, T)
+
+    def V(fn, r, w):
+        tr("V", fn, r, w)
+
+    def ts(out, in0, s1, s2, op0, op1, r, w):
+        if op1 is None:
+            V(lambda e: e.tensor_scalar(out, in0, s1, None, op0), r, w)
+        else:
+            V(lambda e: e.tensor_scalar(out, in0, s1, s2, op0, op1), r, w)
+
+    def tt(out, a, b, op, r, w):
+        V(lambda e: e.tensor_tensor(out, a, b, op), r, w)
+
+    def cp(out, in_, r, w):
+        V(lambda e: e.tensor_copy(out, in_), r, w)
+
+    def scan(out, a, b, init, op0, op1, r, w):
+        V(lambda e: e.tensor_tensor_scan(out, a, b, init, op0, op1), r, w)
+
+    def fill(ap, c, w):
+        V(lambda e: e.memset(ap, c), [], w)
+
+    def act(out, in_, func, r, w, **kw):
+        tr("A", lambda e: e.activation(out, in_, func, **kw), r, w)
+
+    def iota(out, pat, base, cm, w, flag=True):
+        if flag:
+            tr("G", lambda e: e.iota(out, pat, base, cm, allow_small_or_imprecise_dtypes=True), [], w)
+        else:
+            tr("G", lambda e: e.iota(out, pat, base, cm), [], w)
+
+    def select(out, in_, pat, op, base, cm, r, w):
+        tr("G", lambda e: e.affine_select(out, in_, pat, op, 0.0, base, cm), r, w)
+
+    def quant(name, a, b, src, lo, r):
+        V(lambda e: e.quantize_mx(T[name][:, a:b], T[name + "s"][:, a:b], T[src][:, lo:lo + 4 * (b - a)]),
+          r, [name, name + "s"])
+
+    def mm(bank, n, sta, sa, mov, ma, start=True, stop=True):
+        p = "p%d" % bank
+        tr("P", lambda e: e.matmul_mx(T[p][:, 0:n], T[sta][:, sa:sa + 128], T[sta + "s"][:, sa:sa + 128],
+                                      T[mov][:, ma:ma + n], T[mov + "s"][:, ma:ma + n], start, stop),
+           [sta, sta + "s", mov, mov + "s"], [p], acc=not start)
+
+    dma("S", lambda e: e.dma_start(T.x0[:, 0:1280], T.x[:]), ("dx", 16), [], ["x0/x"])
+    dma("A", lambda e: e.dma_start(T.ut[:], T.u[:]), ("du", 16), [], ["ut"])
+    dma("S", lambda e: e.dma_start(T.wq[:].bitcast(dt.uint8), T.wc[:]), ("dw", 32), [], ["wq"])
+    dma("S", lambda e: e.dma_start(T.wqs[:], T.ws[:]), ("dw", 32), [], ["wqs"])
+    dma("S", lambda e: e.dma_start(T.vt[:], T.v[:]), ("dv", 16), [], ["vt"])
+
+    iota(T.pi[:, 0:1], [[0, 1]], 0, 1, ["pi/0"], False)
+    iota(T.xi[:, 0:8], [[16, 8]], 4, 0, ["xi/u"], False)
+    iota(T.i16[:], [[0, 20], [1, 16]], 0, 0, ["i16"])
+    iota(T.i4[:], [[0, 100], [1, 4]], 0, 0, ["i4"])
+    iota(T.ij[:], [[1, 336]], 0, 0, ["ij"])
+    fill(T.one[:], 1.0, ["one"])
+    select(T.id4[:], T.one[:], [[-16, 8], [0, 64]], OP.is_ge, 0, 1, ["one"], ["id4"])
+    select(T.eg[:], T.id4[:], [[16, 8], [0, 64]], OP.is_ge, 15, -1, ["id4"], ["eg"])
+    iota(T.sl1[:, 0:20], [[0, 4], [16, 5]], 0, 0, ["sl1"])
+    iota(T.xi[:, 8:11], [[16, 3]], 0, 0, ["xi/a"], False)
+    iota(T.xi[:, 16:26], [[16, 10]], 0, 0, ["xi/b"], False)
+
+    fill(T.half[:], 0.5, ["half"])
+    cp(T.ul[:], T.xi[:, 0:8], ["xi/u"], ["ul"])
+    ts(T.pi[:, 1:2], T.pi[:, 0:1], 15, None, OP.bitwise_and, None, ["pi/0"], ["pi/1"])
+    ts(T.pi[:, 2:3], T.pi[:, 0:1], 3, None, OP.bitwise_and, None, ["pi/0"], ["pi/2"])
+    ts(T.pi[:, 3:4], T.pi[:, 1:2], 2, None, OP.logical_shift_right, None, ["pi/1"], ["pi/3"])
+    cp(T.pc[:, 0:3], T.pi[:, 1:4], ["pi"], ["pc/0"])
+    ts(T.pc[:, 3:4], T.pc[:, 0:1], -B16, 15 * B16 - 16.0, OP.mult, OP.add, ["pc/0"], ["pc/3"])
+    ts(T.mm[:], T.i16[:], T.pc[:, 0:1], -2.0 * NEG, OP.not_equal, OP.mult, ["i16", "pc/0"], ["mm"])
+    ts(T.d0[:], T.i16[:], 2.0 * NEG, -NEG, OP.mult, OP.add, ["i16"], ["d0"])
+    quant("qu", 0, 128, "ut", 0, ["ut"])
+    cp(T.qur[:].bitcast(dt.uint32), T.qu[:].bitcast(dt.uint32).indirect(T.ul[:, 0:8]), ["qu", "ul"], ["qur"])
+    act(T.rs[:], T.i16[:], AF.Sign, ["i16"], ["rs"])
+    act(T.tb[:, 0:320], T.rs[:], AF.Copy, ["rs"], ["tb"], scale=32 * B16, bias=-33 * B16)
+    act(T.ox[:], T.i4[:], AF.Sign, ["i4"], ["ox"])
+    act(T.wsl[:], T.ox[:], AF.Copy, ["ox"], ["wsl"], scale=8 * B4, bias=-9 * B4)
+    act(T.qurs[:], T.qus[:].indirect(T.ul[:, 0:8]), AF.Copy, ["qus", "ul"], ["qurs"])
+    act(T.on[:], T.i16[:], AF.Copy, ["i16"], ["on"], scale=0.0, bias=UNIT)
+    act(T.cw[:, 0:320], T.i16[:], AF.Copy, ["i16"], ["cw/a"], scale=0.0, bias=0.125 * UNIT)
+    act(T.cw[:, 320:328], T.i16[:, 0:8], AF.Copy, ["i16"], ["cw/b"], scale=0.0, bias=0.125 * UNIT)
+    act(T.wrow[:], T.ij[:], AF.Copy, ["ij"], ["wrow"], scale=0.0, bias=320.0)
+    act(T.iw[:], T.ij[:], AF.Copy, ["ij"], ["iw"], scale=UNIT, bias=0.375 * UNIT)
+    ts(T.ta[:, 0:320], T.i16[:], T.pc[:, 0:1], 2 * B16, OP.is_gt, OP.mult, ["i16", "pc/0"], ["ta"])
+    tt(T.k16[:], T.ta[:, 0:320], T.tb[:, 0:320], OP.add, ["ta", "tb"], ["k16"])
+    fill(T.x0[:, 1280:1296], 0.0, ["x0/z"])
+    for j in range(4):
+        fill(T.lm[:, j:j + 1], (-0.3125 + j / 64.0) * UNIT, ["lm/0"])
+    select(T.id4[:], T.half[:], [[-1, 128], [0, 4]], OP.is_equal, 0, 1, ["half"], ["id4"])
+
+    def unpack_constants():
+        for b in range(4):
+            select(T.un[:, 512 * b:512 * b + 512], T.id4[:], [[0, 128], [1, 4]], OP.is_equal, -b, 0, ["id4"],
+                   ["un/%d" % b])
+
+    def product_constants():
+        ts(T.ta[:], T.i4[:], T.pc[:, 2:3], 2 * B4, OP.is_gt, OP.mult, ["i4", "pc/0"], ["ta"])
+
+    def claim_constants():
+        tt(T.k4[:], T.ta[:], T.wsl[:], OP.add, ["ta", "wsl"], ["k4"])
+        ts(T.sc[:], T.sl1[:, 0:20], T.pc[:, 0:1], 16.125, OP.add, OP.add, ["sl1", "pc/0"], ["sc"])
+        ts(T.sl2[:, 0:3], T.xi[:, 8:11], T.pc[:, 0:1], 13.0, OP.add, OP.mult, ["xi/a", "pc/0"], ["sl2/a"])
+        ts(T.sc[:], T.sc[:], UNIT, None, OP.mult, None, ["sc"], ["sc"])
+        cp(T.xi[:, 28:31], T.sl2[:, 0:3], ["sl2/a"], ["xi/c"])
+        fill(T.btile[:, 1280:1472], 0.0, ["btile/pad"])
+        ts(T.xi[:, 44:47], T.xi[:, 28:31], 6, None, OP.logical_shift_right, None, ["xi/c"], ["xi/e"])
+        ts(T.xi[:, 8:11], T.xi[:, 44:47], 1.0, None, OP.add, None, ["xi/e"], ["xi/a"])
+        ts(T.xi[:, 60:63], T.xi[:, 44:47], 4, None, OP.bitwise_and, None, ["xi/e"], ["xi/g"])
+        ts(T.xi[:, 28:31], T.xi[:, 8:11], 3, None, OP.bitwise_and, None, ["xi/a"], ["xi/c"])
+        tt(T.xi[:, 8:11], T.xi[:, 28:31], T.xi[:, 60:63], OP.add, ["xi/c", "xi/g"], ["xi/a"])
+        cp(T.xl[:, 0:3], T.xi[:, 8:11], ["xi/a"], ["xl"])
+
+    def first_flight_constants():
+        quant("qun", 0, 512, "un", 0, ["un"])
+        fill(T.z0[:, 320:512], 0.0, ["z0/pad"])
+        fill(T.h0[:, 320:512], 0.0, ["h0/pad"])
+
+    def second_flight_constants():
+        ts(T.sl2[:, 4:14], T.xi[:, 16:26], T.pc[:, 0:1], 205.0, OP.add, OP.mult, ["xi/b", "pc/0"], ["sl2/b"])
+        fill(T.bk[:, 1280:1296], 0.0, ["bk/z"])
+        cp(T.xi[:, 32:42], T.sl2[:, 4:14], ["sl2/b"], ["xi/d"])
+        for k in range(4):
+            fill(T.kc[:, 20 * k:20 * k + 20], 80.0 * ((k + 3) % 4) - 320.0, ["kc/%d" % k])
+        ts(T.xi[:, 48:58], T.xi[:, 32:42], 12, None, OP.logical_shift_right, None, ["xi/d"], ["xi/f"])
+        fill(T.x1[:, 1280:1296], 0.0, ["x1/z"])
+        cp(T.l80[:], T.xi[:, 48:58], ["xi/f"], ["l80"])
+
+    gdn = [0]
+    lsn = [0]
+
+    def fused(src, dst, step, sem, reads):
+        for planes in (False, True):
+            trs = []
+            for i in range(3):
+                to = T.cores[(rank + step * (i + 1)) % N]
+                en = topo.engines(core, to)
+                h = len(en) // 8
+                if planes:
+                    en = en[4 * h:6 * h] if i == 0 else en[6 * h:8 * h] if i == 1 else en[0:4 * h]
+                else:
+                    en = en[0:2 * h] if i == 0 else en[2 * h:4 * h] if i == 1 else en[4 * h:8 * h]
+                mask = 0
+                for x in en:
+                    mask |= 1 << x
+                ad = topo.addr(to)
+                a, b = 80 * i, 80 * i + 80
+                if planes:
+                    s_ap, d_ap = T[src + "s"][:, a:b], T[dst + "s"][:, a:b]
+                else:
+                    s_ap, d_ap = T[src][:, a:b].bitcast(dt.uint8), T[dst][:, a:b].bitcast(dt.uint8)
+                trs.append(RemoteDMATransfer(dst_ids=[DstId(rid=ad[0], pnc=ad[1])], dma_engine_mask=mask,
+                                             remote_sem=T.sem[sem], src=s_ap, dst=d_ap))
+                lsn[0] += len(en)
+            remote(lambda e: e.remote_dma_fused(trs, local_sem=T.sem.ls), ("ls", lsn[0]), reads)
+
+    def landed(sem, dst, step):
+        n = 0
+        for i in range(3):
+            h = len(topo.engines(T.cores[(rank - step * (i + 1)) % N], core)) // 8
+            n += (8 if i == 2 else 4) * h
+        arrive((sem, n), [dst, dst + "s"])
+
+    for r in range(NR):
+        X, XN = "x%d" % r, "x%d" % (r + 1)
+        xa, xn = T[X], T[XN]
+        quant("qx", 0, 320, X, 0, [X])
+        mm(0, 320, "qur", 0, "qx", 0)
+        mm(2, 320, "qu", 0, "qx", 0)
+        mm(1, 320, "qur", 0, "qx", 0)
+        if r == 0:
+            product_constants()
+        tt(T.d1[:], T.p0[:, 0:320], T.mm[:], OP.add, ["p0", "mm"], ["d1"])
+        scan(T.st[:], T.d0[:], T.d1[:], -NEG, OP.min, OP.max, ["d0", "d1"], ["st"])
+        act(T.v4[:], T.p2[:, 0:320], AF.Sign, ["p2"], ["v4"])
+        act(T.v4[:], T.v4[:], AF.Relu, ["v4"], ["v4"], scale=UNIT)
+        for b in range(2, 5):
+            a = ACT_COLS[b]
+            n = "ct%d" % b
+            for t in range(4):
+                c = 4 * b + t
+                act(T[n][:, t:4 * a:4], T.p1[:, 0:a], AF.Sign, ["p1", "st"], ["%s/a%d" % (n, t)],
+                    bias=T.st[:, 16 * c + 15:16 * c + 16], scale=-1.0)
+            act(T[n][:, 0:4 * a], T[n][:, 0:4 * a], AF.Relu, ["%s/a%d" % (n, t) for t in range(4)], [n + "/a"])
+        gdn[0] += 16
+        dma("G", lambda e: e.dma_start(T.v4[:], T.ij[:, 0:320], accum_op=OP.add), ("gd", gdn[0]), ["ij"], ["v4"])
+        if r == 0:
+            unpack_constants()
+
+        def compare(b):
+            n, a = "ct%d" % b, ACT_COLS[b]
+            for t in range(4):
+                c = 4 * b + t
+                s = T.st[:, 16 * c + 15:16 * c + 16]
+                if 16 * c > a:
+                    ts(T[n][:, 4 * a + t:64 * c:4], T.p0[:, a:16 * c], s, None, OP.is_lt, None, ["p0", "st"],
+                       ["%s/l%d" % (n, t)])
+                ts(T[n][:, 64 * c + t:1280:4], T.p0[:, 16 * c:320], s, None, OP.is_le, None, ["p0", "st"],
+                   ["%s/u%d" % (n, t)])
+
+        def count(b):
+            n, q = "ct%d" % b, "qc%d" % (b % 3)
+            quant(q, 0, 320, n, 0, [n])
+            mm(3, 320, "qeg", 0, q, 0, b == 0, b == 4)
+        compare(0)
+        if r == 0:
+            quant("qeg", 0, 128, "eg", 0, ["eg"])
+        count(0)
+        compare(1)
+        count(1)
+        compare(2)
+        compare(3)
+        compare(4)
+        tt(T.eq[:], T.p0[:, 0:320], T.st[:], OP.is_equal, ["p0", "st"], ["eq"])
+        count(2)
+        scan(T.rc[:, 0:320], T.rs[:], T.eq[:], 0.0, OP.mult, OP.add, ["rs", "eq"], ["rc"])
+        count(3)
+        ts(T.rcb[:], T.rc[:, 15:320:16], T.pc[:, 3:4], None, OP.add, None, ["rc", "pc/3"], ["rcb"])
+        count(4)
+        scan(T.rx[:], T.k16[:], T.p3[:, 0:320], 0.0, OP.add, OP.max, ["k16", "p3"], ["rx"])
+        tt(T.rk[:], T.rx[:, 15:320:16], T.rcb[:], OP.subtract, ["rx", "rcb"], ["rk"])
+        cp(T.rk16[:], T.rk[:], ["rk"], ["rk16"])
+        cp(T.wrow[:, 0:336].indirect(T.rk16[:, 0:20]), T.v4[:], ["rk16", "v4"], ["wrow"])
+        scan(T.cw[:, 1:321], T.wrow[:, 16:336], T.on[:], 0.125 * UNIT, OP.add, OP.add, ["wrow", "on"], ["cw"])
+        tot = T.cw[:, 320:321]
+        act(T.junk[:], T.cw[:, 0:320], AF.Sign, ["cw"], ["junk", "acc/0"], bias=tot, scale=-4.0,
+            accum_out=T.acc[:, 0:1])
+        if r == 0:
+            claim_constants()
+        sm = T.sm
+
+        def ends(s):
+            ts(T.e16[:, 2 * s:2 * s + 1], T.acc[:, s:s + 1], 0.5, 160.0, OP.mult, OP.add, ["acc/%d" % s],
+               ["e16/%d" % s])
+
+        def show(buf, win, w, s):
+            cp(T[buf][:, 16 * s:16 * s + 16], T[win][:, 0:w].indirect(T.e16[:, 2 * s:2 * s + 1]),
+               [win, "e16/%d" % s], ["%s/%d" % (buf, s)])
+        ke = [sm[:, 0:1], sm[:, 1:2], sm[:, 2:3]]
+        em = [sm[:, 4:8], sm[:, 8:12], sm[:, 12:16]]
+        for s in range(3):
+            m = 4 - s
+            lmc = T.lm[:, 4 * s:4 * s + 4]
+            ends(s)
+            if s < 2:
+                show("gg", "cw", 328, s)
+                tt(sm[:, 16:20], T.gg[:, 16 * s:16 * s + 4], lmc, OP.add, ["gg/%d" % s, "lm/%d" % s], ["sm/gm"])
+                V(lambda e: e.tensor_reduce(sm[:, 20:21], sm[:, 16:20], AxisListType.X, OP.min), ["sm/gm"], ["sm/kg"])
+                ts(sm[:, 21 + s:22 + s], sm[:, 20:21], float(m - 2), tot, OP.mult, OP.add, ["sm/kg", "cw"],
+                   ["sm/th%d" % s])
+                act(T.junk[:], T.cw[:, 0:320], AF.Sign, ["cw", "sm/th%d" % s], ["junk", "acc/%d" % (s + 1)],
+                    bias=sm[:, 21 + s:22 + s], scale=-float(m - 1), accum_out=T.acc[:, s + 1:s + 2])
+            show("ee", "iw", 336, s)
+            tt(em[s], T.ee[:, 16 * s:16 * s + 4], lmc, OP.add, ["ee/%d" % s, "lm/%d" % s], ["sm/em%d" % s])
+            V(lambda e, s=s: e.tensor_reduce(ke[s], em[s], AxisListType.X, OP.min), ["sm/em%d" % s], ["sm/ke%d" % s])
+            w = ["sm/em%d" % s, "sm/ke%d" % s]
+            if s < 2:
+                ts(sm[:, 24:28], em[s], ke[s], 2.0 ** 32, OP.is_equal, OP.mult, w, ["sm/w"])
+                tt(T.lm[:, 4 * s + 4:4 * s + 8], lmc, sm[:, 24:28], OP.add, ["sm/w", "lm/%d" % s],
+                   ["lm/%d" % (s + 1)])
+            if s == 0:
+                ts(sm[:, 28:32], em[0], ke[0], ke[0], OP.is_equal, OP.mult, w, ["sm/n1"])
+                act(T.wsl[:, 320:400], T.wrow[:, 16:96], AF.Copy, ["wrow"], ["wsl/e"])
+            elif s == 1:
+                ts(sm[:, 32:36], em[1], ke[1], ke[0], OP.is_equal, OP.mult, w + ["sm/ke0"], ["sm/f2"])
+                ts(sm[:, 36:40], em[1], ke[1], ke[1], OP.is_equal, OP.mult, w, ["sm/n2"])
+                ts(sm[:, 44:48], T.lm[:, 8:12], 2.0 ** 31, None, OP.is_lt, None, ["lm/2"], ["sm/l3"])
+                tt(sm[:, 40:44], sm[:, 28:32], sm[:, 36:40], OP.add, ["sm/n1", "sm/n2"], ["sm/n12"])
+                ts(sm[:, 48:52], sm[:, 44:48], 320.0625 * UNIT, 16.0 * UNIT, OP.mult, OP.add, ["sm/l3"], ["sm/nl"])
+                tt(sm[:, 52:56], sm[:, 48:52], sm[:, 40:44], OP.add, ["sm/nl", "sm/n12"], ["sm/nb"])
+            else:
+                ts(sm[:, 56:57], ke[2], -1.0, ke[1], OP.mult, OP.add, ["sm/ke2", "sm/ke1"], ["sm/d"])
+                ts(sm[:, 57:58], ke[2], -320.0625 * UNIT, None, OP.add, None, ["sm/ke2"], ["sm/d2"])
+                ts(sm[:, 60:64], sm[:, 44:48], ke[2], None, OP.mult, None, ["sm/l3", "sm/ke2"], ["sm/lk"])
+                ts(sm[:, 64:68], em[2], ke[2], sm[:, 56:57], OP.is_equal, OP.mult, w + ["sm/d"], ["sm/fa"])
+                ts(sm[:, 68:72], em[2], ke[2], sm[:, 57:58], OP.is_equal, OP.mult, w + ["sm/d2"], ["sm/na"])
+                tt(sm[:, 72:76], sm[:, 60:64], sm[:, 32:36], OP.add, ["sm/lk", "sm/f2"], ["sm/f"])
+                tt(T.tab[:, 4:8], sm[:, 52:56], sm[:, 68:72], OP.add, ["sm/nb", "sm/na"], ["tab/n"])
+                tt(T.tab[:, 0:4], sm[:, 72:76], sm[:, 64:68], OP.add, ["sm/f", "sm/fa"], ["tab/f"])
+        tabs = ["tab/f", "tab/n"]
+        cp(T.te[:], T.tab[:, 0:8].indirect(T.xl[:, 0:3]), tabs + ["xl"], ["te"])
+        tt(T.pl[:, 0:20], T.te[:, 0:20], T.sc[:], OP.add, ["te", "sc"], ["pl/a"])
+        tt(T.pl[:, 20:40], T.pl[:, 0:20], T.te[:, 20:40], OP.is_lt, ["pl/a", "te"], ["pl/b"])
+        tt(T.pl[:, 40:60], T.pl[:, 0:20], T.pl[:, 20:40], OP.mult, ["pl/a", "pl/b"], ["pl/c"])
+        ts(T.off16[:], T.pl[:, 40:60], 1.0 / UNIT, None, OP.mult, None, ["pl/c"], ["off16"])
+        cp(T.wsl[:, 0:320], T.wrow[:, 0:336].indirect(T.off16[:, 0:20]), ["wrow", "off16"], ["wsl/s"])
+        scan(T.ox[:], T.k4[:], T.wsl[:], 0.0, OP.add, OP.max, ["k4", "wsl"], ["ox"])
+        cp(T.oi[:, 0:100], T.ox[:, 3:400:4], ["ox"], ["oi/a"])
+        ts(T.oi[:, 100:200], T.oi[:, 0:100], 511, None, OP.bitwise_and, None, ["oi/a"], ["oi/b"])
+        ts(T.off4[:], T.oi[:, 100:200], 4.0, T.pc[:, 1:2], OP.mult, OP.add, ["oi/b", "pc/0"], ["off4"])
+        win = xa[:, 0:1296]
+
+        def take(eng, lo, n):
+            o, i = T.btile[:, 4 * lo:4 * lo + 4 * n], win.indirect(T.off4[:, lo // 4:(lo + n) // 4])
+            k = ["btile/%d" % lo]
+            if eng == "V":
+                cp(o, i, [X, "off4"], k)
+            else:
+                act(o, i, AF.Copy, [X, "off4"], k)
+        take("A", 0, 120)
+        take("V", 120, 120)
+        qb, qh, came, back = "qb%d" % r, "qh%d" % r, "came%d" % r, "back%d" % r
+        quant(qb, 0, 240, "btile", 0, ["btile/0", "btile/120"])
+        fused(qb, came, 1, "ab%d" % r, [qb, qb + "s"])
+        landed("ab%d" % r, came, 1)
+        if r == 0:
+            first_flight_constants()
+        take("A", 240, 80)
+        quant("qbo", 0, 128, "btile", 960, ["btile/240", "btile/pad"])
+        act(T.eh[:, 0:320], win.indirect(T.off4[:, 80:100]), AF.Copy, [X, "off4"], ["eh/0"], scale=0.5)
+        for b in range(4):
+            mm(4 + b, 128, "qun", 128 * b, "qbo", 0)
+        for b in range(4):
+            tt(T.z0[:, b:320:4], T["p%d" % (4 + b)][:, 0:80], T.eh[:, b:320:4], OP.add, ["p%d" % (4 + b), "eh/0"],
+               ["z0/%d" % b])
+        act(T.eh[:, 320:640], T.eh[:, 0:320], AF.Copy, ["eh/0"], ["eh/1"])
+        act(T.eh[:, 640:960], T.eh[:, 0:320], AF.Copy, ["eh/0"], ["eh/2"])
+        quant("qzo", 0, 128, "z0", 0, ["z0"])
+        for b in range(4):
+            mm(b, 128, "wq", 128 * b, "qzo", 0)
+        for b in range(4):
+            act(T.h0[:, b:320:4], T["p%d" % b][:, 0:80], AF.Copy, ["p%d" % b], ["h0/%d" % b], scale=0.03125)
+        for b in range(4):
+            mm(4 + b, 240, "qun", 128 * b, came, 0)
+        for b in range(4):
+            tt(T.z1[:, b:960:4], T["p%d" % (4 + b)][:, 0:240], T.eh[:, b:960:4], OP.add, ["p%d" % (4 + b), "eh"],
+               ["z1/%d" % b])
+        quant("qz1", 0, 240, "z1", 0, ["z1"])
+        for b in range(4):
+            mm(b, 240, "wq", 128 * b, "qz1", 0)
+        for b in range(4):
+            o, i = T.h1[:, b:960:4], T["p%d" % b][:, 0:240]
+            if b % 2:
+                ts(o, i, 0.03125, None, OP.mult, None, ["p%d" % b], ["h1/%d" % b])
+            else:
+                act(o, i, AF.Copy, ["p%d" % b], ["h1/%d" % b], scale=0.03125)
+        quant(qh, 0, 240, "h1", 0, ["h1"])
+        fused(qh, back, -1, "ah%d" % r, [qh, qh + "s"])
+        landed("ah%d" % r, back, -1)
+        quant("qho", 0, 128, "h0", 0, ["h0"])
+        for b in range(4):
+            mm(4 + b, 128, "qun", 128 * b, "qho", 0)
+        if r == 0:
+            second_flight_constants()
+        ts(sm[:, 80:84], T.tab[:, 4:8], -16.0 * UNIT, None, OP.add, None, tabs, ["sm/la"])
+        ts(sm[:, 84:88], T.tab[:, 0:4], 80.0 * UNIT, None, OP.add, None, tabs, ["sm/lb"])
+        cp(T.tab[:, 8:12], T.tab[:, 0:4], tabs, ["tab/g"])
+        tt(T.tab[:, 12:16], sm[:, 80:84], sm[:, 84:88], OP.min, ["sm/la", "sm/lb"], ["tab/l"])
+        for k in range(4):
+            ts(T.rks[:, 20 * k:20 * k + 20], T.rk[:], -15.875, UNIT, OP.add, OP.mult, ["rk"], ["rks/%d" % k])
+        cp(T.tf[:], T.tab[:, 8:16].indirect(T.l80[:, 0:10]), ["tab/g", "tab/l", "l80"], ["tf"])
+        s1, s2 = T.sl1, T.sl2
+        tt(s1[:, 0:80], T.rks[:], T.tf[:, 80:160], OP.is_lt, ["rks", "tf"], ["sl1/a"])
+        tt(s1[:, 80:160], T.rks[:], T.tf[:, 0:80], OP.is_ge, ["rks", "tf"], ["sl1/b"])
+        tt(s1[:, 160:240], T.rks[:], T.tf[:, 0:80], OP.subtract, ["rks", "tf"], ["sl1/c"])
+        tt(s1[:, 240:320], s1[:, 0:80], s1[:, 80:160], OP.mult, ["sl1/a", "sl1/b"], ["sl1/d"])
+        ts(s1[:, 320:400], s1[:, 160:240], 1.0 / UNIT, None, OP.mult, None, ["sl1/c"], ["sl1/e"])
+        tt(T.pl[:], s1[:, 320:400], T.kc[:], OP.add, ["sl1/e", "kc"], ["pl"])
+        tt(s1[:, 0:80], T.pl[:], s1[:, 240:320], OP.mult, ["pl", "sl1/d"], ["sl1/a"])
+        tt(s2[:, 0:40], s1[:, 0:40], s1[:, 40:80], OP.add, ["sl1/a"], ["sl2/a"])
+        tt(s2[:, 40:60], s2[:, 0:20], s2[:, 20:40], OP.add, ["sl2/a"], ["sl2/b"])
+        ts(s2[:, 60:80], s2[:, 40:60], 320.0, None, OP.add, None, ["sl2/b"], ["sl2/c"])
+        cp(T.po[:], s2[:, 60:80], ["sl2/c"], ["po"])
+        for t in range(4):
+            ts(T.po16[:, 20 * t:20 * t + 20], T.po[:], 4.0, float(t), OP.mult, OP.add, ["po"], ["po16/%d" % t])
+        for b in range(4):
+            o, i = T.bk[:, 960 + b:1280:4], T["p%d" % (4 + b)][:, 0:80]
+            act(o, i, AF.Copy, ["p%d" % (4 + b)], ["bk/own%d" % b], scale=2.0)
+        if r == NR - 1:
+            ts(T.rc[:, 0:240], T.ij[:, 0:240], 80.0, None, OP.add, None, ["ij"], ["rc/a"])
+            ts(T.rc[:, 240:320], T.ij[:, 240:320], -240.0, None, OP.add, None, ["ij"], ["rc/b"])
+            fill(T.rc[:, 320:336], -1.0, ["rc/c"])
+            cp(T.po16[:, 80:100], T.po[:], ["po"], ["po16/s"])
+            act(T.eq[:], T.rc[:, 0:336].indirect(T.po16[:, 80:100]), AF.Copy, ["rc", "po16/s"], ["eq"])
+            for q in range(8):
+                dma("S", lambda e, q=q: e.dma_start(T.sl[q:q + 1, :], T.eq[16 * q:16 * q + 1, :]), ("out", 0),
+                    ["eq"], [])
+            quant("qv", 0, 128, "vt", 0, ["vt"])
+        for b in range(4):
+            mm(b, 240, "qun", 128 * b, back, 0)
+        for b in range(4):
+            o, i = T.bk[:, b:960:4], T["p%d" % b][:, 0:240]
+            if b % 2:
+                ts(o, i, 2.0, None, OP.mult, None, ["p%d" % b], ["bk/%d" % b])
+            else:
+                act(o, i, AF.Copy, ["p%d" % b], ["bk/%d" % b], scale=2.0)
+        for t in range(4):
+            tt(xn[:, t:1280:4], T.bk[:, 0:1296].indirect(T.po16[:, 20 * t:20 * t + 20]), xa[:, t:1280:4], OP.add,
+               ["bk", "po16/%d" % t, X], [XN + "/x%d" % t])
+
+    X = "x%d" % NR
+    quant("qx", 0, 320, X, 0, [X + "/x%d" % t for t in range(4)])
+    mm(4, 320, "qv", 0, "qx", 0)
+    dma("S", lambda e: e.dma_start(T.oc[:], T.qx[:].bitcast(dt.uint8)), ("out", 0), ["qx"], [])
+    for k in range(4):
+        dma("S", lambda e, k=k: e.dma_start(T.osc[4 * k:4 * k + 4, :], T.qxs[32 * k:32 * k + 4, :]), ("out", 0),
+            ["qxs"], [])
+    act(T.d1[:], T.p4[:, 0:320], AF.Copy, ["p4"], ["d1"])
+    dma("A", lambda e: e.dma_start(T.y[:], T.d1[:]), ("out", 0), ["d1"], [])
+    g.wait_ge(T.sem.out, 16 * (8 + 1 + 4 + 1))
+    g.wait_ge(T.sem.ls, lsn[0])

@@ -7,7 +7,6 @@ UNIT = 2.0 ** 20
 NEG = 2.0 ** 97
 B16 = 1024.0
 B4 = 2.0 ** 21
-ACT_COLS = [0, 0, 128, 192, 256]
 
 
 def _scratch():
@@ -21,18 +20,18 @@ def _scratch():
         s[n] = ("sbuf", [128, w], F8)
         s[n + "s"] = ("sbuf", [128, w], U8)
     sb(BF, x0=1296, x1=1296, x2=1296, ut=512, vt=512, eg=512, one=512, half=512, id4=512, un=2048, btile=1472, eh=960,
-       z0=512, h0=512, z1=960, h1=960, bk=1296, junk=320)
-    for b in range(5):
-        sb(BF, **{"ct%d" % b: 1280})
+       z0=512, h0=512, z1=960, h1=960, bk=1296, junk=1280, ct0=1280, ct1=1280, ct2=1280)
     for n, w in (("qu", 128), ("qur", 128), ("qv", 128), ("wq", 512), ("qx", 320), ("qeg", 128), ("qun", 512),
-                 ("qbo", 128), ("qzo", 128), ("qho", 128), ("qz1", 240), ("qc0", 320), ("qc1", 320), ("qc2", 320)):
+                 ("qbo", 128), ("qzo", 128), ("qho", 128), ("qz1", 240), ("qb", 240), ("qh", 240),
+                 ("qc0", 320), ("qc1", 320), ("qc2", 320)):
         code(n, w)
     for r in range(NR):
-        for n in ("qb", "qh", "came", "back"):
+        for n in ("came", "back"):
             code("%s%d" % (n, r), 240)
     sb(F32, i16=320, i4=400, ij=336, mm=320, d0=320, rs=320, k16=320, k4=400, ta=400, tb=400, d1=320,
-       st=320, eq=320, rc=336, rcb=20, pc=8, v4=320, wrow=336, cw=328, on=320, rx=320, rk=20, acc=8, gg=48, ee=48,
-       iw=336, lm=16, sm=128, tab=16, te=48, sc=20, pl=80, wsl=400, ox=400, tf=160, rks=80, kc=80, sl1=400, sl2=80)
+       st=320, eq=320, rc=336, rcb=20, pc=8, v4=320, wrow=336, cw=328, on=320, rx=320, rk=20, acc=8, rsum=32, ncq=20,
+       gg=48, ee=48, iw=336, lm=24, sm=128, tab=16, te=48, sc=20, pl=80, wsl=400, ox=400, tf=160, rks=80, kc=80,
+       sl1=400, sl2=80)
     sb(I32, pi=8, xi=64, oi=200, po=20)
     sb(U16, ul=8, xl=4, l80=10, rk16=20, e16=8, off16=20, off4=100, po16=100)
     for b in range(8):
@@ -41,8 +40,8 @@ def _scratch():
 
 
 SCRATCH = _scratch()
-SEMAPHORES = (["sV", "sA", "sP", "sG", "gd", "ls", "dx", "du", "dw", "dv", "out"]
-              + ["ab%d" % r for r in range(NR)] + ["ah%d" % r for r in range(NR)])
+SEMAPHORES = (["sV", "sA", "sP", "sG", "gd", "lqb", "lqh", "dx", "du", "dw", "dv", "out"]
+              + [p + str(r) for p in ("came", "back") for r in range(NR)])
 
 
 def tracker(g, T):
@@ -187,32 +186,32 @@ def rank_program(g, core, T, topo):
     iota(T.xi[:, 8:11], [[16, 3]], 0, 0, ["xi/a"], False)
     iota(T.xi[:, 16:26], [[16, 10]], 0, 0, ["xi/b"], False)
 
-    fill(T.half[:], 0.5, ["half"])
     cp(T.ul[:], T.xi[:, 0:8], ["xi/u"], ["ul"])
     ts(T.pi[:, 1:2], T.pi[:, 0:1], 15, None, OP.bitwise_and, None, ["pi/0"], ["pi/1"])
     ts(T.pi[:, 2:3], T.pi[:, 0:1], 3, None, OP.bitwise_and, None, ["pi/0"], ["pi/2"])
     ts(T.pi[:, 3:4], T.pi[:, 1:2], 2, None, OP.logical_shift_right, None, ["pi/1"], ["pi/3"])
     cp(T.pc[:, 0:3], T.pi[:, 1:4], ["pi"], ["pc/0"])
-    ts(T.pc[:, 3:4], T.pc[:, 0:1], -B16, 15 * B16 - 16.0, OP.mult, OP.add, ["pc/0"], ["pc/3"])
     ts(T.mm[:], T.i16[:], T.pc[:, 0:1], -2.0 * NEG, OP.not_equal, OP.mult, ["i16", "pc/0"], ["mm"])
     ts(T.d0[:], T.i16[:], 2.0 * NEG, -NEG, OP.mult, OP.add, ["i16"], ["d0"])
-    quant("qu", 0, 128, "ut", 0, ["ut"])
-    cp(T.qur[:].bitcast(dt.uint32), T.qu[:].bitcast(dt.uint32).indirect(T.ul[:, 0:8]), ["qu", "ul"], ["qur"])
     act(T.rs[:], T.i16[:], AF.Sign, ["i16"], ["rs"])
     act(T.tb[:, 0:320], T.rs[:], AF.Copy, ["rs"], ["tb"], scale=32 * B16, bias=-33 * B16)
-    act(T.ox[:], T.i4[:], AF.Sign, ["i4"], ["ox"])
-    act(T.wsl[:], T.ox[:], AF.Copy, ["ox"], ["wsl"], scale=8 * B4, bias=-9 * B4)
-    act(T.qurs[:], T.qus[:].indirect(T.ul[:, 0:8]), AF.Copy, ["qus", "ul"], ["qurs"])
+    ts(T.ta[:, 0:320], T.i16[:], T.pc[:, 0:1], 2 * B16, OP.is_gt, OP.mult, ["i16", "pc/0"], ["ta"])
+    tt(T.k16[:], T.ta[:, 0:320], T.tb[:, 0:320], OP.add, ["ta", "tb"], ["k16"])
+    quant("qu", 0, 128, "ut", 0, ["ut"])
+    cp(T.qur[:].bitcast(dt.uint32), T.qu[:].bitcast(dt.uint32).indirect(T.ul[:, 0:8]), ["qu", "ul"], ["qur"])
     act(T.on[:], T.i16[:], AF.Copy, ["i16"], ["on"], scale=0.0, bias=UNIT)
     act(T.cw[:, 0:320], T.i16[:], AF.Copy, ["i16"], ["cw/a"], scale=0.0, bias=0.125 * UNIT)
     act(T.cw[:, 320:328], T.i16[:, 0:8], AF.Copy, ["i16"], ["cw/b"], scale=0.0, bias=0.125 * UNIT)
+    act(T.qurs[:], T.qus[:].indirect(T.ul[:, 0:8]), AF.Copy, ["qus", "ul"], ["qurs"])
+    act(T.ct2[:, 3:1280:4], T.i16[:], AF.Copy, ["i16"], ["ct2/n"], scale=0.0)
+    act(T.half[:], T.one[:], AF.Copy, ["one"], ["half"], scale=0.5)
+    for c in range(10):
+        act(T["ct%d" % (c // 4)][:, 64 * c + c % 4:64 * c + 64:4], T.i16[:, 0:16], AF.Copy, ["i16"],
+            ["ct%d/h%d" % (c // 4, c)], scale=0.0)
+    act(T.ox[:], T.i4[:], AF.Sign, ["i4"], ["ox"])
+    act(T.wsl[:], T.ox[:], AF.Copy, ["ox"], ["wsl"], scale=8 * B4, bias=-9 * B4)
     act(T.wrow[:], T.ij[:], AF.Copy, ["ij"], ["wrow"], scale=0.0, bias=320.0)
-    act(T.iw[:], T.ij[:], AF.Copy, ["ij"], ["iw"], scale=UNIT, bias=0.375 * UNIT)
-    ts(T.ta[:, 0:320], T.i16[:], T.pc[:, 0:1], 2 * B16, OP.is_gt, OP.mult, ["i16", "pc/0"], ["ta"])
-    tt(T.k16[:], T.ta[:, 0:320], T.tb[:, 0:320], OP.add, ["ta", "tb"], ["k16"])
     fill(T.x0[:, 1280:1296], 0.0, ["x0/z"])
-    for j in range(4):
-        fill(T.lm[:, j:j + 1], (-0.3125 + j / 64.0) * UNIT, ["lm/0"])
     select(T.id4[:], T.half[:], [[-1, 128], [0, 4]], OP.is_equal, 0, 1, ["half"], ["id4"])
 
     def unpack_constants():
@@ -221,16 +220,26 @@ def rank_program(g, core, T, topo):
                    ["un/%d" % b])
 
     def product_constants():
-        ts(T.ta[:], T.i4[:], T.pc[:, 2:3], 2 * B4, OP.is_gt, OP.mult, ["i4", "pc/0"], ["ta"])
+        for j in range(4):
+            fill(T.lm[:, j:j + 1], (-0.3125 + j / 64.0) * UNIT, ["lm/0"])
+        fill(T.rsum[:, 19:21], 0.0, ["rsum/z"])
+
+    def order_constants():
+        ts(T.pc[:, 3:4], T.pc[:, 0:1], 1.0 - B16, 15 * B16 - 191.0, OP.mult, OP.add, ["pc/0"], ["pc/3"])
+        ts(T.pc[:, 4:5], T.pc[:, 0:1], 1.0 - B16, 15 * B16 - 175.0, OP.mult, OP.add, ["pc/0"], ["pc/4"])
+        ts(T.ncq[:, 0:10], T.i4[:, 0:10], 0.0, T.pc[:, 3:4], OP.mult, OP.add, ["i4", "pc/3"], ["ncq/a"])
+        ts(T.ncq[:, 10:20], T.i4[:, 0:10], 0.0, T.pc[:, 4:5], OP.mult, OP.add, ["i4", "pc/4"], ["ncq/b"])
 
     def claim_constants():
-        tt(T.k4[:], T.ta[:], T.wsl[:], OP.add, ["ta", "wsl"], ["k4"])
-        ts(T.sc[:], T.sl1[:, 0:20], T.pc[:, 0:1], 16.125, OP.add, OP.add, ["sl1", "pc/0"], ["sc"])
+        act(T.iw[:], T.ij[:], AF.Copy, ["ij"], ["iw"], scale=UNIT, bias=0.375 * UNIT)
+        ts(T.ta[:], T.i4[:], T.pc[:, 2:3], 2 * B4, OP.is_gt, OP.mult, ["i4", "pc/0"], ["ta"])
         ts(T.sl2[:, 0:3], T.xi[:, 8:11], T.pc[:, 0:1], 13.0, OP.add, OP.mult, ["xi/a", "pc/0"], ["sl2/a"])
-        ts(T.sc[:], T.sc[:], UNIT, None, OP.mult, None, ["sc"], ["sc"])
+        ts(T.sc[:], T.sl1[:, 0:20], T.pc[:, 0:1], 16.125, OP.add, OP.add, ["sl1", "pc/0"], ["sc"])
         cp(T.xi[:, 28:31], T.sl2[:, 0:3], ["sl2/a"], ["xi/c"])
-        fill(T.btile[:, 1280:1472], 0.0, ["btile/pad"])
+        tt(T.k4[:], T.ta[:], T.wsl[:], OP.add, ["ta", "wsl"], ["k4"])
         ts(T.xi[:, 44:47], T.xi[:, 28:31], 6, None, OP.logical_shift_right, None, ["xi/c"], ["xi/e"])
+        ts(T.sc[:], T.sc[:], UNIT, None, OP.mult, None, ["sc"], ["sc"])
+        fill(T.btile[:, 1280:1472], 0.0, ["btile/pad"])
         ts(T.xi[:, 8:11], T.xi[:, 44:47], 1.0, None, OP.add, None, ["xi/e"], ["xi/a"])
         ts(T.xi[:, 60:63], T.xi[:, 44:47], 4, None, OP.bitwise_and, None, ["xi/e"], ["xi/g"])
         ts(T.xi[:, 28:31], T.xi[:, 8:11], 3, None, OP.bitwise_and, None, ["xi/a"], ["xi/c"])
@@ -252,10 +261,11 @@ def rank_program(g, core, T, topo):
         fill(T.x1[:, 1280:1296], 0.0, ["x1/z"])
         cp(T.l80[:], T.xi[:, 48:58], ["xi/f"], ["l80"])
 
-    gdn = [0]
-    lsn = [0]
+    gdn, jn = [0], [0]
+    lsn = {"qb": 0, "qh": 0}
 
-    def fused(src, dst, step, sem, reads):
+    def send(src, dst, step):
+        got = 0
         for planes in (False, True):
             trs = []
             for i in range(3):
@@ -276,16 +286,12 @@ def rank_program(g, core, T, topo):
                 else:
                     s_ap, d_ap = T[src][:, a:b].bitcast(dt.uint8), T[dst][:, a:b].bitcast(dt.uint8)
                 trs.append(RemoteDMATransfer(dst_ids=[DstId(rid=ad[0], pnc=ad[1])], dma_engine_mask=mask,
-                                             remote_sem=T.sem[sem], src=s_ap, dst=d_ap))
-                lsn[0] += len(en)
-            remote(lambda e: e.remote_dma_fused(trs, local_sem=T.sem.ls), ("ls", lsn[0]), reads)
-
-    def landed(sem, dst, step):
-        n = 0
-        for i in range(3):
-            h = len(topo.engines(T.cores[(rank - step * (i + 1)) % N], core)) // 8
-            n += (8 if i == 2 else 4) * h
-        arrive((sem, n), [dst, dst + "s"])
+                                             remote_sem=T.sem[dst], src=s_ap, dst=d_ap))
+                lsn[src] += len(en)
+                got += len(en)
+            remote(lambda e: e.remote_dma_fused(trs, local_sem=T.sem["l" + src]), ("l" + src, lsn[src]),
+                   [src + "s"] if planes else [src])
+        arrive((dst, got), [dst, dst + "s"])
 
     for r in range(NR):
         X, XN = "x%d" % r, "x%d" % (r + 1)
@@ -293,67 +299,64 @@ def rank_program(g, core, T, topo):
         quant("qx", 0, 320, X, 0, [X])
         mm(0, 320, "qur", 0, "qx", 0)
         mm(2, 320, "qu", 0, "qx", 0)
-        mm(1, 320, "qur", 0, "qx", 0)
         if r == 0:
             product_constants()
         tt(T.d1[:], T.p0[:, 0:320], T.mm[:], OP.add, ["p0", "mm"], ["d1"])
         scan(T.st[:], T.d0[:], T.d1[:], -NEG, OP.min, OP.max, ["d0", "d1"], ["st"])
         act(T.v4[:], T.p2[:, 0:320], AF.Sign, ["p2"], ["v4"])
         act(T.v4[:], T.v4[:], AF.Relu, ["v4"], ["v4"], scale=UNIT)
-        for b in range(2, 5):
-            a = ACT_COLS[b]
-            n = "ct%d" % b
-            for t in range(4):
-                c = 4 * b + t
-                act(T[n][:, t:4 * a:4], T.p1[:, 0:a], AF.Sign, ["p1", "st"], ["%s/a%d" % (n, t)],
-                    bias=T.st[:, 16 * c + 15:16 * c + 16], scale=-1.0)
-            act(T[n][:, 0:4 * a], T[n][:, 0:4 * a], AF.Relu, ["%s/a%d" % (n, t) for t in range(4)], [n + "/a"])
         gdn[0] += 16
         dma("G", lambda e: e.dma_start(T.v4[:], T.ij[:, 0:320], accum_op=OP.add), ("gd", gdn[0]), ["ij"], ["v4"])
         if r == 0:
             unpack_constants()
 
-        def compare(b):
-            n, a = "ct%d" % b, ACT_COLS[b]
-            for t in range(4):
-                c = 4 * b + t
-                s = T.st[:, 16 * c + 15:16 * c + 16]
-                if 16 * c > a:
-                    ts(T[n][:, 4 * a + t:64 * c:4], T.p0[:, a:16 * c], s, None, OP.is_lt, None, ["p0", "st"],
-                       ["%s/l%d" % (n, t)])
-                ts(T[n][:, 64 * c + t:1280:4], T.p0[:, 16 * c:320], s, None, OP.is_le, None, ["p0", "st"],
-                   ["%s/u%d" % (n, t)])
+        def compare(c):
+            n, t = "ct%d" % (c // 4), c % 4
+            for (k, lo, hi, op, col) in ((c, c + 1, c + 11, OP.is_le, c), (c + 10, c + 11, 20, OP.is_le, 10 + c),
+                                         (c + 10, 0, c, OP.is_lt, 20 + c)):
+                if lo < hi:
+                    o, key = T[n][:, 64 * lo + t:64 * hi:4], "%s/%d" % (n, col)
+                    ts(o, T.p0[:, 16 * lo:16 * hi], T.st[:, 16 * k + 15:16 * k + 16], None, op, None, ["p0", "st"],
+                       [key])
+                    jn[0] = (jn[0] + 1) % 8
+                    act(T.junk[:, 160 * jn[0]:160 * jn[0] + 16 * (hi - lo)], o, AF.Copy, [key],
+                        ["junk/%d" % jn[0], "rsum/%d" % col], accum_out=T.rsum[:, col:col + 1])
 
         def count(b):
-            n, q = "ct%d" % b, "qc%d" % (b % 3)
-            quant(q, 0, 320, n, 0, [n])
-            mm(3, 320, "qeg", 0, q, 0, b == 0, b == 4)
-        compare(0)
+            quant("qc%d" % b, 0, 320, "ct%d" % b, 0, ["ct%d" % b])
+            mm(3, 320, "qeg", 0, "qc%d" % b, 0, b == 0, b == 2)
+        for c in range(4):
+            compare(c)
         if r == 0:
             quant("qeg", 0, 128, "eg", 0, ["eg"])
         count(0)
-        compare(1)
+        if r == 0:
+            order_constants()
+        for c in range(4, 8):
+            compare(c)
         count(1)
-        compare(2)
-        compare(3)
-        compare(4)
-        tt(T.eq[:], T.p0[:, 0:320], T.st[:], OP.is_equal, ["p0", "st"], ["eq"])
+        tt(T.ct2[:, 2:1280:4], T.st[:], T.p0[:, 0:320], OP.is_ge, ["p0", "st"], ["ct2/d"])
+        compare(8)
+        compare(9)
         count(2)
-        scan(T.rc[:, 0:320], T.rs[:], T.eq[:], 0.0, OP.mult, OP.add, ["rs", "eq"], ["rc"])
-        count(3)
-        ts(T.rcb[:], T.rc[:, 15:320:16], T.pc[:, 3:4], None, OP.add, None, ["rc", "pc/3"], ["rcb"])
-        count(4)
+        scan(T.rc[:, 0:320], T.rs[:], T.ct2[:, 2:1280:4], 0.0, OP.mult, OP.add, ["rs", "ct2/d"], ["rc"])
+        tt(T.rcb[:], T.rc[:, 15:320:16], T.ncq[:], OP.add, ["rc", "ncq"], ["rcb"])
+        tt(T.rcb[:], T.rcb[:], T.rsum[:, 0:20], OP.add, ["rcb", "rsum/z"] + ["rsum/%d" % c for c in range(19)], ["rcb"])
+        tt(T.rcb[:, 10:20], T.rcb[:, 10:20], T.rsum[:, 20:30], OP.add,
+           ["rcb", "rsum/z"] + ["rsum/%d" % c for c in range(21, 30)], ["rcb"])
         scan(T.rx[:], T.k16[:], T.p3[:, 0:320], 0.0, OP.add, OP.max, ["k16", "p3"], ["rx"])
         tt(T.rk[:], T.rx[:, 15:320:16], T.rcb[:], OP.subtract, ["rx", "rcb"], ["rk"])
         cp(T.rk16[:], T.rk[:], ["rk"], ["rk16"])
         cp(T.wrow[:, 0:336].indirect(T.rk16[:, 0:20]), T.v4[:], ["rk16", "v4"], ["wrow"])
         scan(T.cw[:, 1:321], T.wrow[:, 16:336], T.on[:], 0.125 * UNIT, OP.add, OP.add, ["wrow", "on"], ["cw"])
         tot = T.cw[:, 320:321]
-        act(T.junk[:], T.cw[:, 0:320], AF.Sign, ["cw"], ["junk", "acc/0"], bias=tot, scale=-4.0,
+        act(T.junk[:, 0:320], T.cw[:, 0:320], AF.Sign, ["cw"], ["junk/0", "junk/1", "acc/0"], bias=tot, scale=-4.0,
             accum_out=T.acc[:, 0:1])
+        sm, lm = T.sm, T.lm
+        ts(sm[:, 20:21], tot, 0.5, None, OP.mult, None, ["cw"], ["sm/t2"])
+        ts(lm[:, 12:16], lm[:, 0:4], sm[:, 20:21], None, OP.add, None, ["lm/0", "sm/t2"], ["lm/t0"])
         if r == 0:
             claim_constants()
-        sm = T.sm
 
         def ends(s):
             ts(T.e16[:, 2 * s:2 * s + 1], T.acc[:, s:s + 1], 0.5, 160.0, OP.mult, OP.add, ["acc/%d" % s],
@@ -366,34 +369,39 @@ def rank_program(g, core, T, topo):
         em = [sm[:, 4:8], sm[:, 8:12], sm[:, 12:16]]
         for s in range(3):
             m = 4 - s
-            lmc = T.lm[:, 4 * s:4 * s + 4]
+            lmc = lm[:, 4 * s:4 * s + 4]
             ends(s)
             if s < 2:
                 show("gg", "cw", 328, s)
-                tt(sm[:, 16:20], T.gg[:, 16 * s:16 * s + 4], lmc, OP.add, ["gg/%d" % s, "lm/%d" % s], ["sm/gm"])
-                V(lambda e: e.tensor_reduce(sm[:, 20:21], sm[:, 16:20], AxisListType.X, OP.min), ["sm/gm"], ["sm/kg"])
-                ts(sm[:, 21 + s:22 + s], sm[:, 20:21], float(m - 2), tot, OP.mult, OP.add, ["sm/kg", "cw"],
-                   ["sm/th%d" % s])
-                act(T.junk[:], T.cw[:, 0:320], AF.Sign, ["cw", "sm/th%d" % s], ["junk", "acc/%d" % (s + 1)],
-                    bias=sm[:, 21 + s:22 + s], scale=-float(m - 1), accum_out=T.acc[:, s + 1:s + 2])
+                tt(sm[:, 16:20], T.gg[:, 16 * s:16 * s + 4], lm[:, 12 + 4 * s:16 + 4 * s], OP.add,
+                   ["gg/%d" % s, "lm/t%d" % s], ["sm/gm"])
+                V(lambda e, s=s: e.tensor_reduce(sm[:, 21 + s:22 + s], sm[:, 16:20], AxisListType.X, OP.min),
+                  ["sm/gm"], ["sm/th%d" % s])
+                act(T.junk[:, 320 * s + 320:320 * s + 640], T.cw[:, 0:320], AF.Sign, ["cw", "sm/th%d" % s],
+                    ["junk/%d" % (2 * s + 2), "junk/%d" % (2 * s + 3), "acc/%d" % (s + 1)],
+                    bias=sm[:, 21 + s:22 + s], scale=-float(m - 1) / (m - 2), accum_out=T.acc[:, s + 1:s + 2])
+                ts(sm[:, 24:28], sm[:, 16:20], sm[:, 21 + s:22 + s], 2.0 ** 32, OP.is_equal, OP.mult,
+                   ["sm/gm", "sm/th%d" % s], ["sm/w"])
             show("ee", "iw", 336, s)
+            if s < 2:
+                tt(lm[:, 4 * s + 4:4 * s + 8], lmc, sm[:, 24:28], OP.add, ["sm/w", "lm/%d" % s],
+                   ["lm/%d" % (s + 1)])
             tt(em[s], T.ee[:, 16 * s:16 * s + 4], lmc, OP.add, ["ee/%d" % s, "lm/%d" % s], ["sm/em%d" % s])
+            if s == 0:
+                ts(lm[:, 16:20], lm[:, 4:8], tot, None, OP.add, None, ["lm/1", "cw"], ["lm/t1"])
+            if s == 1:
+                ts(sm[:, 44:48], lm[:, 8:12], 2.0 ** 31, None, OP.is_lt, None, ["lm/2"], ["sm/l3"])
             V(lambda e, s=s: e.tensor_reduce(ke[s], em[s], AxisListType.X, OP.min), ["sm/em%d" % s], ["sm/ke%d" % s])
             w = ["sm/em%d" % s, "sm/ke%d" % s]
-            if s < 2:
-                ts(sm[:, 24:28], em[s], ke[s], 2.0 ** 32, OP.is_equal, OP.mult, w, ["sm/w"])
-                tt(T.lm[:, 4 * s + 4:4 * s + 8], lmc, sm[:, 24:28], OP.add, ["sm/w", "lm/%d" % s],
-                   ["lm/%d" % (s + 1)])
             if s == 0:
-                ts(sm[:, 28:32], em[0], ke[0], ke[0], OP.is_equal, OP.mult, w, ["sm/n1"])
                 act(T.wsl[:, 320:400], T.wrow[:, 16:96], AF.Copy, ["wrow"], ["wsl/e"])
             elif s == 1:
-                ts(sm[:, 32:36], em[1], ke[1], ke[0], OP.is_equal, OP.mult, w + ["sm/ke0"], ["sm/f2"])
-                ts(sm[:, 36:40], em[1], ke[1], ke[1], OP.is_equal, OP.mult, w, ["sm/n2"])
-                ts(sm[:, 44:48], T.lm[:, 8:12], 2.0 ** 31, None, OP.is_lt, None, ["lm/2"], ["sm/l3"])
-                tt(sm[:, 40:44], sm[:, 28:32], sm[:, 36:40], OP.add, ["sm/n1", "sm/n2"], ["sm/n12"])
                 ts(sm[:, 48:52], sm[:, 44:48], 320.0625 * UNIT, 16.0 * UNIT, OP.mult, OP.add, ["sm/l3"], ["sm/nl"])
-                tt(sm[:, 52:56], sm[:, 48:52], sm[:, 40:44], OP.add, ["sm/nl", "sm/n12"], ["sm/nb"])
+                ts(sm[:, 28:32], em[0], ke[0], ke[0], OP.is_equal, OP.mult, ["sm/em0", "sm/ke0"], ["sm/n1"])
+                ts(sm[:, 36:40], em[1], ke[1], ke[1], OP.is_equal, OP.mult, w, ["sm/n2"])
+                tt(sm[:, 40:44], sm[:, 28:32], sm[:, 48:52], OP.add, ["sm/n1", "sm/nl"], ["sm/n12"])
+                ts(sm[:, 32:36], em[1], ke[1], ke[0], OP.is_equal, OP.mult, w + ["sm/ke0"], ["sm/f2"])
+                tt(sm[:, 52:56], sm[:, 40:44], sm[:, 36:40], OP.add, ["sm/n12", "sm/n2"], ["sm/nb"])
             else:
                 ts(sm[:, 56:57], ke[2], -1.0, ke[1], OP.mult, OP.add, ["sm/ke2", "sm/ke1"], ["sm/d"])
                 ts(sm[:, 57:58], ke[2], -320.0625 * UNIT, None, OP.add, None, ["sm/ke2"], ["sm/d2"])
@@ -423,12 +431,11 @@ def rank_program(g, core, T, topo):
                 cp(o, i, [X, "off4"], k)
             else:
                 act(o, i, AF.Copy, [X, "off4"], k)
+        came, back = "came%d" % r, "back%d" % r
         take("A", 0, 120)
         take("V", 120, 120)
-        qb, qh, came, back = "qb%d" % r, "qh%d" % r, "came%d" % r, "back%d" % r
-        quant(qb, 0, 240, "btile", 0, ["btile/0", "btile/120"])
-        fused(qb, came, 1, "ab%d" % r, [qb, qb + "s"])
-        landed("ab%d" % r, came, 1)
+        quant("qb", 0, 240, "btile", 0, ["btile/0", "btile/120"])
+        send("qb", came, 1)
         if r == 0:
             first_flight_constants()
         take("A", 240, 80)
@@ -460,9 +467,8 @@ def rank_program(g, core, T, topo):
                 ts(o, i, 0.03125, None, OP.mult, None, ["p%d" % b], ["h1/%d" % b])
             else:
                 act(o, i, AF.Copy, ["p%d" % b], ["h1/%d" % b], scale=0.03125)
-        quant(qh, 0, 240, "h1", 0, ["h1"])
-        fused(qh, back, -1, "ah%d" % r, [qh, qh + "s"])
-        landed("ah%d" % r, back, -1)
+        quant("qh", 0, 240, "h1", 0, ["h1"])
+        send("qh", back, -1)
         quant("qho", 0, 128, "h0", 0, ["h0"])
         for b in range(4):
             mm(4 + b, 128, "qun", 128 * b, "qho", 0)
@@ -524,4 +530,5 @@ def rank_program(g, core, T, topo):
     act(T.d1[:], T.p4[:, 0:320], AF.Copy, ["p4"], ["d1"])
     dma("A", lambda e: e.dma_start(T.y[:], T.d1[:]), ("out", 0), ["d1"], [])
     g.wait_ge(T.sem.out, 16 * (8 + 1 + 4 + 1))
-    g.wait_ge(T.sem.ls, lsn[0])
+    for n in sorted(lsn):
+        g.wait_ge(T.sem["l" + n], lsn[n])

from concourse.bass import DstId, RemoteDMATransfer
from concourse.mybir import dt, AluOpType as OP, AxisListType, ActivationFunctionType as AF

F32, BF, I32, U16, U8, F8 = "float32", "bfloat16", "int32", "uint16", "uint8", "float8_e4m3fn_x4"
NR = 2
UNIT = 2.0 ** 20
NEG = 2.0 ** 97
B16 = 1024.0
B4 = 2.0 ** 21


def _scratch():
    s = {}

    def sb(dtype, **kw):
        for n in kw:
            s[n] = ("sbuf", [128, kw[n]], dtype)

    def code(n, w):
        s[n] = ("sbuf", [128, w], F8)
        s[n + "s"] = ("sbuf", [128, w], U8)
    sb(BF, x0=1296, x1=1296, x2=1296, ut=512, vt=512, eg=512, one=512, half=512, id4=512, un=2048, btile=1472, eh=960,
       z0=512, h0=512, z1=960, h1=960, bk=1296, junk=1280, ct0=1280, ct1=1280, ct2=1280)
    for n, w in (("qu", 128), ("qur", 128), ("qv", 128), ("wq", 512), ("qx", 320), ("qeg", 128), ("qun", 512),
                 ("qbo", 128), ("qzo", 128), ("qho", 128), ("qz1", 240), ("qb", 240), ("qh", 240),
                 ("qc0", 320), ("qc1", 320), ("qc2", 320)):
        code(n, w)
    for r in range(NR):
        for n in ("came", "back"):
            code("%s%d" % (n, r), 240)
    sb(F32, i16=320, i4=400, ij=336, mm=320, d0=320, rs=320, k16=320, k4=400, ta=400, tb=400, d1=320,
       st=320, eq=320, rc=336, rcb=20, pc=8, v4=320, wrow=336, cw=328, on=320, rx=320, rk=20, acc=8, rsum=32, ncq=20,
       gg=48, ee=48, iw=336, lm=24, sm=128, tab=16, te=48, sc=20, pl=80, wsl=400, ox=400, tf=160, rks=80, kc=80,
       sl1=400, sl2=80)
    sb(I32, pi=8, xi=64, oi=200, po=20)
    sb(U16, ul=8, xl=4, l80=10, rk16=20, e16=8, off16=20, off4=100, po16=100)
    for b in range(8):
        s["p%d" % b] = ("psum", [128, 512], F32)
    return s


SCRATCH = _scratch()
SEMAPHORES = (["sV", "sA", "sP", "sG", "gd", "lqb", "lqh", "dx", "du", "dw", "dv", "out"]
              + [p + str(r) for p in ("came", "back") for r in range(NR)])


def tracker(g, T):
    eng = {"V": g.vector, "A": g.scalar, "P": g.tensor, "G": g, "S": g.sync}
    sem = {"V": "sV", "A": "sA", "P": "sP", "G": "sG"}
    count = {q: 0 for q in sem}
    known = {q: {} for q in eng}
    known["far"] = {}
    clock = {}
    log = {}

    def split(k):
        a = k.split("/")
        return a[0], (a[1] if len(a) > 1 else None)

    def need(q, reads, writes, acc):
        out = {}
        for keys, w in ((reads, False), (writes, True)):
            for k in keys:
                n, s = split(k)
                psum = n[0] == "p" and n[1:].isdigit()
                for (s2, q2, tok, w2) in log.get(n, []):
                    if not psum and s is not None and s2 is not None and s != s2:
                        continue
                    dma = tok[0] not in ("sV", "sA", "sP", "sG")
                    if q2 == q and not dma:
                        if (not w2 and not w) or (acc and w):
                            continue
                    elif not w and not w2 and not psum:
                        continue
                    out[tok[0]] = max(out.get(tok[0], 0), tok[1])
        return out

    def wait(q, toks):
        for s in sorted(toks):
            if known[q].get(s, 0) < toks[s]:
                eng[q].wait_ge(T.sem[s], toks[s])
                for (s2, v2) in clock.get((s, toks[s]), {}).items():
                    known[q][s2] = max(known[q].get(s2, 0), v2)
                known[q][s] = max(known[q].get(s, 0), toks[s])

    def note(q, tok, reads, writes):
        c = dict(known[q])
        c[tok[0]] = max(c.get(tok[0], 0), tok[1])
        if tok in clock:
            for s2 in clock[tok]:
                c[s2] = max(c.get(s2, 0), clock[tok][s2])
        clock[tok] = c
        for k in writes:
            n, s = split(k)
            log[n] = [e for e in log.get(n, []) if not (s is None or e[0] == s)] + [(s, q, tok, True)]
        for k in reads:
            n, s = split(k)
            log[n] = [e for e in log.get(n, []) if not (not e[3] and e[1] == q and e[0] == s)] + [(s, q, tok, False)]

    def tr(q, fn, reads, writes, acc=False):
        wait(q, need(q, reads, writes, acc))
        count[q] += 1
        fn(eng[q]).then_inc(T.sem[sem[q]], 1)
        note(q, (sem[q], count[q]), reads, writes)

    def dma(q, fn, tok, reads, writes):
        wait(q, need(q, reads, writes, False))
        fn(eng[q]).then_inc(T.sem[tok[0]], 16)
        note(q, tok, reads, writes)

    def remote(fn, tok, reads):
        wait("G", need("G", reads, [], False))
        fn(g)
        note("G", tok, reads, [])

    def arrive(tok, writes):
        note("far", tok, [], writes)
    return tr, dma, remote, arrive


def rank_program(g, core, T, topo):
    rank = T.rank_of(core)
    if rank is None:
        return
    N = len(T.cores)
    tr, dma, remote, arrive = tracker(g, T)

    def V(fn, r, w):
        tr("V", fn, r, w)

    def ts(out, in0, s1, s2, op0, op1, r, w):
        if op1 is None:
            V(lambda e: e.tensor_scalar(out, in0, s1, None, op0), r, w)
        else:
            V(lambda e: e.tensor_scalar(out, in0, s1, s2, op0, op1), r, w)

    def tt(out, a, b, op, r, w):
        V(lambda e: e.tensor_tensor(out, a, b, op), r, w)

    def cp(out, in_, r, w):
        V(lambda e: e.tensor_copy(out, in_), r, w)

    def scan(out, a, b, init, op0, op1, r, w):
        V(lambda e: e.tensor_tensor_scan(out, a, b, init, op0, op1), r, w)

    def fill(ap, c, w):
        V(lambda e: e.memset(ap, c), [], w)

    def act(out, in_, func, r, w, **kw):
        tr("A", lambda e: e.activation(out, in_, func, **kw), r, w)

    def iota(out, pat, base, cm, w, flag=True):
        if flag:
            tr("G", lambda e: e.iota(out, pat, base, cm, allow_small_or_imprecise_dtypes=True), [], w)
        else:
            tr("G", lambda e: e.iota(out, pat, base, cm), [], w)

    def select(out, in_, pat, op, base, cm, r, w):
        tr("G", lambda e: e.affine_select(out, in_, pat, op, 0.0, base, cm), r, w)

    def quant(name, a, b, src, lo, r):
        V(lambda e: e.quantize_mx(T[name][:, a:b], T[name + "s"][:, a:b], T[src][:, lo:lo + 4 * (b - a)]),
          r, [name, name + "s"])

    def mm(bank, n, sta, sa, mov, ma, start=True, stop=True):
        p = "p%d" % bank
        tr("P", lambda e: e.matmul_mx(T[p][:, 0:n], T[sta][:, sa:sa + 128], T[sta + "s"][:, sa:sa + 128],
                                      T[mov][:, ma:ma + n], T[mov + "s"][:, ma:ma + n], start, stop),
           [sta, sta + "s", mov, mov + "s"], [p], acc=not start)

    dma("S", lambda e: e.dma_start(T.x0[:, 0:1280], T.x[:]), ("dx", 16), [], ["x0/x"])
    dma("A", lambda e: e.dma_start(T.ut[:], T.u[:]), ("du", 16), [], ["ut"])
    dma("S", lambda e: e.dma_start(T.wq[:].bitcast(dt.uint8), T.wc[:]), ("dw", 32), [], ["wq"])
    dma("S", lambda e: e.dma_start(T.wqs[:], T.ws[:]), ("dw", 32), [], ["wqs"])
    dma("S", lambda e: e.dma_start(T.vt[:], T.v[:]), ("dv", 16), [], ["vt"])

    iota(T.pi[:, 0:1], [[0, 1]], 0, 1, ["pi/0"], False)
    iota(T.xi[:, 0:8], [[16, 8]], 4, 0, ["xi/u"], False)
    iota(T.i16[:], [[0, 20], [1, 16]], 0, 0, ["i16"])
    iota(T.i4[:], [[0, 100], [1, 4]], 0, 0, ["i4"])
    iota(T.ij[:], [[1, 336]], 0, 0, ["ij"])
    fill(T.one[:], 1.0, ["one"])
    select(T.id4[:], T.one[:], [[-16, 8], [0, 64]], OP.is_ge, 0, 1, ["one"], ["id4"])
    select(T.eg[:], T.id4[:], [[16, 8], [0, 64]], OP.is_ge, 15, -1, ["id4"], ["eg"])
    iota(T.sl1[:, 0:20], [[0, 4], [16, 5]], 0, 0, ["sl1"])
    iota(T.xi[:, 8:11], [[16, 3]], 0, 0, ["xi/a"], False)
    iota(T.xi[:, 16:26], [[16, 10]], 0, 0, ["xi/b"], False)

    cp(T.ul[:], T.xi[:, 0:8], ["xi/u"], ["ul"])
    ts(T.pi[:, 1:2], T.pi[:, 0:1], 15, None, OP.bitwise_and, None, ["pi/0"], ["pi/1"])
    ts(T.pi[:, 2:3], T.pi[:, 0:1], 3, None, OP.bitwise_and, None, ["pi/0"], ["pi/2"])
    ts(T.pi[:, 3:4], T.pi[:, 1:2], 2, None, OP.logical_shift_right, None, ["pi/1"], ["pi/3"])
    cp(T.pc[:, 0:3], T.pi[:, 1:4], ["pi"], ["pc/0"])
    ts(T.mm[:], T.i16[:], T.pc[:, 0:1], -2.0 * NEG, OP.not_equal, OP.mult, ["i16", "pc/0"], ["mm"])
    ts(T.d0[:], T.i16[:], 2.0 * NEG, -NEG, OP.mult, OP.add, ["i16"], ["d0"])
    act(T.rs[:], T.i16[:], AF.Sign, ["i16"], ["rs"])
    act(T.tb[:, 0:320], T.rs[:], AF.Copy, ["rs"], ["tb"], scale=32 * B16, bias=-33 * B16)
    ts(T.ta[:, 0:320], T.i16[:], T.pc[:, 0:1], 2 * B16, OP.is_gt, OP.mult, ["i16", "pc/0"], ["ta"])
    tt(T.k16[:], T.ta[:, 0:320], T.tb[:, 0:320], OP.add, ["ta", "tb"], ["k16"])
    quant("qu", 0, 128, "ut", 0, ["ut"])
    cp(T.qur[:].bitcast(dt.uint32), T.qu[:].bitcast(dt.uint32).indirect(T.ul[:, 0:8]), ["qu", "ul"], ["qur"])
    act(T.on[:], T.i16[:], AF.Copy, ["i16"], ["on"], scale=0.0, bias=UNIT)
    act(T.cw[:, 0:320], T.i16[:], AF.Copy, ["i16"], ["cw/a"], scale=0.0, bias=0.125 * UNIT)
    act(T.cw[:, 320:328], T.i16[:, 0:8], AF.Copy, ["i16"], ["cw/b"], scale=0.0, bias=0.125 * UNIT)
    act(T.qurs[:], T.qus[:].indirect(T.ul[:, 0:8]), AF.Copy, ["qus", "ul"], ["qurs"])
    act(T.ct2[:, 3:1280:4], T.i16[:], AF.Copy, ["i16"], ["ct2/n"], scale=0.0)
    act(T.half[:], T.one[:], AF.Copy, ["one"], ["half"], scale=0.5)
    for c in range(10):
        act(T["ct%d" % (c // 4)][:, 64 * c + c % 4:64 * c + 64:4], T.i16[:, 0:16], AF.Copy, ["i16"],
            ["ct%d/h%d" % (c // 4, c)], scale=0.0)
    act(T.ox[:], T.i4[:], AF.Sign, ["i4"], ["ox"])
    act(T.wsl[:], T.ox[:], AF.Copy, ["ox"], ["wsl"], scale=8 * B4, bias=-9 * B4)
    act(T.wrow[:], T.ij[:], AF.Copy, ["ij"], ["wrow"], scale=0.0, bias=320.0)
    fill(T.x0[:, 1280:1296], 0.0, ["x0/z"])
    select(T.id4[:], T.half[:], [[-1, 128], [0, 4]], OP.is_equal, 0, 1, ["half"], ["id4"])

    def unpack_constants():
        for b in range(4):
            select(T.un[:, 512 * b:512 * b + 512], T.id4[:], [[0, 128], [1, 4]], OP.is_equal, -b, 0, ["id4"],
                   ["un/%d" % b])

    def product_constants():
        for j in range(4):
            fill(T.lm[:, j:j + 1], (-0.3125 + j / 64.0) * UNIT, ["lm/0"])
        fill(T.rsum[:, 19:21], 0.0, ["rsum/z"])

    def order_constants():
        ts(T.pc[:, 3:4], T.pc[:, 0:1], 1.0 - B16, 15 * B16 - 191.0, OP.mult, OP.add, ["pc/0"], ["pc/3"])
        ts(T.pc[:, 4:5], T.pc[:, 0:1], 1.0 - B16, 15 * B16 - 175.0, OP.mult, OP.add, ["pc/0"], ["pc/4"])
        ts(T.ncq[:, 0:10], T.i4[:, 0:10], 0.0, T.pc[:, 3:4], OP.mult, OP.add, ["i4", "pc/3"], ["ncq/a"])
        ts(T.ncq[:, 10:20], T.i4[:, 0:10], 0.0, T.pc[:, 4:5], OP.mult, OP.add, ["i4", "pc/4"], ["ncq/b"])

    def claim_constants():
        act(T.iw[:], T.ij[:], AF.Copy, ["ij"], ["iw"], scale=UNIT, bias=0.375 * UNIT)
        ts(T.ta[:], T.i4[:], T.pc[:, 2:3], 2 * B4, OP.is_gt, OP.mult, ["i4", "pc/0"], ["ta"])
        ts(T.sl2[:, 0:3], T.xi[:, 8:11], T.pc[:, 0:1], 13.0, OP.add, OP.mult, ["xi/a", "pc/0"], ["sl2/a"])
        ts(T.sc[:], T.sl1[:, 0:20], T.pc[:, 0:1], 16.125, OP.add, OP.add, ["sl1", "pc/0"], ["sc"])
        cp(T.xi[:, 28:31], T.sl2[:, 0:3], ["sl2/a"], ["xi/c"])
        tt(T.k4[:], T.ta[:], T.wsl[:], OP.add, ["ta", "wsl"], ["k4"])
        ts(T.xi[:, 44:47], T.xi[:, 28:31], 6, None, OP.logical_shift_right, None, ["xi/c"], ["xi/e"])
        ts(T.sc[:], T.sc[:], UNIT, None, OP.mult, None, ["sc"], ["sc"])
        fill(T.btile[:, 1280:1472], 0.0, ["btile/pad"])
        ts(T.xi[:, 8:11], T.xi[:, 44:47], 1.0, None, OP.add, None, ["xi/e"], ["xi/a"])
        ts(T.xi[:, 60:63], T.xi[:, 44:47], 4, None, OP.bitwise_and, None, ["xi/e"], ["xi/g"])
        ts(T.xi[:, 28:31], T.xi[:, 8:11], 3, None, OP.bitwise_and, None, ["xi/a"], ["xi/c"])
        tt(T.xi[:, 8:11], T.xi[:, 28:31], T.xi[:, 60:63], OP.add, ["xi/c", "xi/g"], ["xi/a"])
        cp(T.xl[:, 0:3], T.xi[:, 8:11], ["xi/a"], ["xl"])

    def first_flight_constants():
        quant("qun", 0, 512, "un", 0, ["un"])
        fill(T.z0[:, 320:512], 0.0, ["z0/pad"])
        fill(T.h0[:, 320:512], 0.0, ["h0/pad"])

    def second_flight_constants():
        ts(T.sl2[:, 4:14], T.xi[:, 16:26], T.pc[:, 0:1], 205.0, OP.add, OP.mult, ["xi/b", "pc/0"], ["sl2/b"])
        fill(T.bk[:, 1280:1296], 0.0, ["bk/z"])
        cp(T.xi[:, 32:42], T.sl2[:, 4:14], ["sl2/b"], ["xi/d"])
        for k in range(4):
            fill(T.kc[:, 20 * k:20 * k + 20], 80.0 * ((k + 3) % 4) - 320.0, ["kc/%d" % k])
        ts(T.xi[:, 48:58], T.xi[:, 32:42], 12, None, OP.logical_shift_right, None, ["xi/d"], ["xi/f"])
        fill(T.x1[:, 1280:1296], 0.0, ["x1/z"])
        cp(T.l80[:], T.xi[:, 48:58], ["xi/f"], ["l80"])

    gdn, jn = [0], [0]
    lsn = {"qb": 0, "qh": 0}

    def send(src, dst, step):
        got = 0
        for planes in (False, True):
            trs = []
            for i in range(3):
                to = T.cores[(rank + step * (i + 1)) % N]
                en = topo.engines(core, to)
                h = len(en) // 8
                if planes:
                    en = en[4 * h:6 * h] if i == 0 else en[6 * h:8 * h] if i == 1 else en[0:4 * h]
                else:
                    en = en[0:2 * h] if i == 0 else en[2 * h:4 * h] if i == 1 else en[4 * h:8 * h]
                mask = 0
                for x in en:
                    mask |= 1 << x
                ad = topo.addr(to)
                a, b = 80 * i, 80 * i + 80
                if planes:
                    s_ap, d_ap = T[src + "s"][:, a:b], T[dst + "s"][:, a:b]
                else:
                    s_ap, d_ap = T[src][:, a:b].bitcast(dt.uint8), T[dst][:, a:b].bitcast(dt.uint8)
                trs.append(RemoteDMATransfer(dst_ids=[DstId(rid=ad[0], pnc=ad[1])], dma_engine_mask=mask,
                                             remote_sem=T.sem[dst], src=s_ap, dst=d_ap))
                lsn[src] += len(en)
                got += len(en)
            remote(lambda e: e.remote_dma_fused(trs, local_sem=T.sem["l" + src]), ("l" + src, lsn[src]),
                   [src + "s"] if planes else [src])
        arrive((dst, got), [dst, dst + "s"])

    for r in range(NR):
        X, XN = "x%d" % r, "x%d" % (r + 1)
        xa, xn = T[X], T[XN]
        quant("qx", 0, 320, X, 0, [X])
        mm(0, 320, "qur", 0, "qx", 0)
        mm(2, 320, "qu", 0, "qx", 0)
        if r == 0:
            product_constants()
        tt(T.d1[:], T.p0[:, 0:320], T.mm[:], OP.add, ["p0", "mm"], ["d1"])
        scan(T.st[:], T.d0[:], T.d1[:], -NEG, OP.min, OP.max, ["d0", "d1"], ["st"])
        act(T.v4[:], T.p2[:, 0:320], AF.Sign, ["p2"], ["v4"])
        act(T.v4[:], T.v4[:], AF.Relu, ["v4"], ["v4"], scale=UNIT)
        gdn[0] += 16
        dma("G", lambda e: e.dma_start(T.v4[:], T.ij[:, 0:320], accum_op=OP.add), ("gd", gdn[0]), ["ij"], ["v4"])
        if r == 0:
            unpack_constants()

        def compare(c):
            n, t = "ct%d" % (c // 4), c % 4
            for (k, lo, hi, op, col) in ((c, c + 1, c + 11, OP.is_le, c), (c + 10, c + 11, 20, OP.is_le, 10 + c),
                                         (c + 10, 0, c, OP.is_lt, 20 + c)):
                if lo < hi:
                    o, key = T[n][:, 64 * lo + t:64 * hi:4], "%s/%d" % (n, col)
                    ts(o, T.p0[:, 16 * lo:16 * hi], T.st[:, 16 * k + 15:16 * k + 16], None, op, None, ["p0", "st"],
                       [key])
                    jn[0] = (jn[0] + 1) % 8
                    act(T.junk[:, 160 * jn[0]:160 * jn[0] + 16 * (hi - lo)], o, AF.Copy, [key],
                        ["junk/%d" % jn[0], "rsum/%d" % col], accum_out=T.rsum[:, col:col + 1])

        def count(b):
            quant("qc%d" % b, 0, 320, "ct%d" % b, 0, ["ct%d" % b])
            mm(3, 320, "qeg", 0, "qc%d" % b, 0, b == 0, b == 2)
        for c in range(4):
            compare(c)
        if r == 0:
            quant("qeg", 0, 128, "eg", 0, ["eg"])
        count(0)
        if r == 0:
            order_constants()
        for c in range(4, 8):
            compare(c)
        count(1)
        tt(T.ct2[:, 2:1280:4], T.st[:], T.p0[:, 0:320], OP.is_ge, ["p0", "st"], ["ct2/d"])
        compare(8)
        compare(9)
        count(2)
        scan(T.rc[:, 0:320], T.rs[:], T.ct2[:, 2:1280:4], 0.0, OP.mult, OP.add, ["rs", "ct2/d"], ["rc"])
        tt(T.rcb[:], T.rc[:, 15:320:16], T.ncq[:], OP.add, ["rc", "ncq"], ["rcb"])
        tt(T.rcb[:], T.rcb[:], T.rsum[:, 0:20], OP.add, ["rcb", "rsum/z"] + ["rsum/%d" % c for c in range(19)], ["rcb"])
        tt(T.rcb[:, 10:20], T.rcb[:, 10:20], T.rsum[:, 20:30], OP.add,
           ["rcb", "rsum/z"] + ["rsum/%d" % c for c in range(21, 30)], ["rcb"])
        scan(T.rx[:], T.k16[:], T.p3[:, 0:320], 0.0, OP.add, OP.max, ["k16", "p3"], ["rx"])
        tt(T.rk[:], T.rx[:, 15:320:16], T.rcb[:], OP.subtract, ["rx", "rcb"], ["rk"])
        cp(T.rk16[:], T.rk[:], ["rk"], ["rk16"])
        cp(T.wrow[:, 0:336].indirect(T.rk16[:, 0:20]), T.v4[:], ["rk16", "v4"], ["wrow"])
        scan(T.cw[:, 1:321], T.wrow[:, 16:336], T.on[:], 0.125 * UNIT, OP.add, OP.add, ["wrow", "on"], ["cw"])
        tot = T.cw[:, 320:321]
        act(T.junk[:, 0:320], T.cw[:, 0:320], AF.Sign, ["cw"], ["junk/0", "junk/1", "acc/0"], bias=tot, scale=-4.0,
            accum_out=T.acc[:, 0:1])
        sm, lm = T.sm, T.lm
        ts(sm[:, 20:21], tot, 0.5, None, OP.mult, None, ["cw"], ["sm/t2"])
        ts(lm[:, 12:16], lm[:, 0:4], sm[:, 20:21], None, OP.add, None, ["lm/0", "sm/t2"], ["lm/t0"])
        if r == 0:
            claim_constants()

        def ends(s):
            ts(T.e16[:, 2 * s:2 * s + 1], T.acc[:, s:s + 1], 0.5, 160.0, OP.mult, OP.add, ["acc/%d" % s],
               ["e16/%d" % s])

        def show(buf, win, w, s):
            cp(T[buf][:, 16 * s:16 * s + 16], T[win][:, 0:w].indirect(T.e16[:, 2 * s:2 * s + 1]),
               [win, "e16/%d" % s], ["%s/%d" % (buf, s)])
        ke = [sm[:, 0:1], sm[:, 1:2], sm[:, 2:3]]
        em = [sm[:, 4:8], sm[:, 8:12], sm[:, 12:16]]
        for s in range(3):
            m = 4 - s
            lmc = lm[:, 4 * s:4 * s + 4]
            ends(s)
            if s < 2:
                show("gg", "cw", 328, s)
                tt(sm[:, 16:20], T.gg[:, 16 * s:16 * s + 4], lm[:, 12 + 4 * s:16 + 4 * s], OP.add,
                   ["gg/%d" % s, "lm/t%d" % s], ["sm/gm"])
                V(lambda e, s=s: e.tensor_reduce(sm[:, 21 + s:22 + s], sm[:, 16:20], AxisListType.X, OP.min),
                  ["sm/gm"], ["sm/th%d" % s])
                act(T.junk[:, 320 * s + 320:320 * s + 640], T.cw[:, 0:320], AF.Sign, ["cw", "sm/th%d" % s],
                    ["junk/%d" % (2 * s + 2), "junk/%d" % (2 * s + 3), "acc/%d" % (s + 1)],
                    bias=sm[:, 21 + s:22 + s], scale=-float(m - 1) / (m - 2), accum_out=T.acc[:, s + 1:s + 2])
                ts(sm[:, 24:28], sm[:, 16:20], sm[:, 21 + s:22 + s], 2.0 ** 32, OP.is_equal, OP.mult,
                   ["sm/gm", "sm/th%d" % s], ["sm/w"])
            show("ee", "iw", 336, s)
            if s < 2:
                tt(lm[:, 4 * s + 4:4 * s + 8], lmc, sm[:, 24:28], OP.add, ["sm/w", "lm/%d" % s],
                   ["lm/%d" % (s + 1)])
            tt(em[s], T.ee[:, 16 * s:16 * s + 4], lmc, OP.add, ["ee/%d" % s, "lm/%d" % s], ["sm/em%d" % s])
            if s == 0:
                ts(lm[:, 16:20], lm[:, 4:8], tot, None, OP.add, None, ["lm/1", "cw"], ["lm/t1"])
            if s == 1:
                ts(sm[:, 44:48], lm[:, 8:12], 2.0 ** 31, None, OP.is_lt, None, ["lm/2"], ["sm/l3"])
            V(lambda e, s=s: e.tensor_reduce(ke[s], em[s], AxisListType.X, OP.min), ["sm/em%d" % s], ["sm/ke%d" % s])
            w = ["sm/em%d" % s, "sm/ke%d" % s]
            if s == 0:
                act(T.wsl[:, 320:400], T.wrow[:, 16:96], AF.Copy, ["wrow"], ["wsl/e"])
            elif s == 1:
                ts(sm[:, 48:52], sm[:, 44:48], 320.0625 * UNIT, 16.0 * UNIT, OP.mult, OP.add, ["sm/l3"], ["sm/nl"])
                ts(sm[:, 28:32], em[0], ke[0], ke[0], OP.is_equal, OP.mult, ["sm/em0", "sm/ke0"], ["sm/n1"])
                ts(sm[:, 36:40], em[1], ke[1], ke[1], OP.is_equal, OP.mult, w, ["sm/n2"])
                tt(sm[:, 40:44], sm[:, 28:32], sm[:, 48:52], OP.add, ["sm/n1", "sm/nl"], ["sm/n12"])
                ts(sm[:, 32:36], em[1], ke[1], ke[0], OP.is_equal, OP.mult, w + ["sm/ke0"], ["sm/f2"])
                tt(sm[:, 52:56], sm[:, 40:44], sm[:, 36:40], OP.add, ["sm/n12", "sm/n2"], ["sm/nb"])
            else:
                ts(sm[:, 56:57], ke[2], -1.0, ke[1], OP.mult, OP.add, ["sm/ke2", "sm/ke1"], ["sm/d"])
                ts(sm[:, 57:58], ke[2], -320.0625 * UNIT, None, OP.add, None, ["sm/ke2"], ["sm/d2"])
                ts(sm[:, 60:64], sm[:, 44:48], ke[2], None, OP.mult, None, ["sm/l3", "sm/ke2"], ["sm/lk"])
                ts(sm[:, 64:68], em[2], ke[2], sm[:, 56:57], OP.is_equal, OP.mult, w + ["sm/d"], ["sm/fa"])
                ts(sm[:, 68:72], em[2], ke[2], sm[:, 57:58], OP.is_equal, OP.mult, w + ["sm/d2"], ["sm/na"])
                tt(sm[:, 72:76], sm[:, 60:64], sm[:, 32:36], OP.add, ["sm/lk", "sm/f2"], ["sm/f"])
                tt(T.tab[:, 4:8], sm[:, 52:56], sm[:, 68:72], OP.add, ["sm/nb", "sm/na"], ["tab/n"])
                tt(T.tab[:, 0:4], sm[:, 72:76], sm[:, 64:68], OP.add, ["sm/f", "sm/fa"], ["tab/f"])
        tabs = ["tab/f", "tab/n"]
        cp(T.te[:], T.tab[:, 0:8].indirect(T.xl[:, 0:3]), tabs + ["xl"], ["te"])
        tt(T.pl[:, 0:20], T.te[:, 0:20], T.sc[:], OP.add, ["te", "sc"], ["pl/a"])
        tt(T.pl[:, 20:40], T.pl[:, 0:20], T.te[:, 20:40], OP.is_lt, ["pl/a", "te"], ["pl/b"])
        tt(T.pl[:, 40:60], T.pl[:, 0:20], T.pl[:, 20:40], OP.mult, ["pl/a", "pl/b"], ["pl/c"])
        ts(T.off16[:], T.pl[:, 40:60], 1.0 / UNIT, None, OP.mult, None, ["pl/c"], ["off16"])
        cp(T.wsl[:, 0:320], T.wrow[:, 0:336].indirect(T.off16[:, 0:20]), ["wrow", "off16"], ["wsl/s"])
        scan(T.ox[:], T.k4[:], T.wsl[:], 0.0, OP.add, OP.max, ["k4", "wsl"], ["ox"])
        cp(T.oi[:, 0:100], T.ox[:, 3:400:4], ["ox"], ["oi/a"])
        ts(T.oi[:, 100:200], T.oi[:, 0:100], 511, None, OP.bitwise_and, None, ["oi/a"], ["oi/b"])
        ts(T.off4[:], T.oi[:, 100:200], 4.0, T.pc[:, 1:2], OP.mult, OP.add, ["oi/b", "pc/0"], ["off4"])
        win = xa[:, 0:1296]

        def take(eng, lo, n):
            o, i = T.btile[:, 4 * lo:4 * lo + 4 * n], win.indirect(T.off4[:, lo // 4:(lo + n) // 4])
            k = ["btile/%d" % lo]
            if eng == "V":
                cp(o, i, [X, "off4"], k)
            else:
                act(o, i, AF.Copy, [X, "off4"], k)
        came, back = "came%d" % r, "back%d" % r
        take("A", 0, 120)
        take("V", 120, 120)
        quant("qb", 0, 240, "btile", 0, ["btile/0", "btile/120"])
        send("qb", came, 1)
        if r == 0:
            first_flight_constants()
        take("A", 240, 80)
        quant("qbo", 0, 128, "btile", 960, ["btile/240", "btile/pad"])
        act(T.eh[:, 0:320], win.indirect(T.off4[:, 80:100]), AF.Copy, [X, "off4"], ["eh/0"], scale=0.5)
        for b in range(4):
            mm(4 + b, 128, "qun", 128 * b, "qbo", 0)
        for b in range(4):
            tt(T.z0[:, b:320:4], T["p%d" % (4 + b)][:, 0:80], T.eh[:, b:320:4], OP.add, ["p%d" % (4 + b), "eh/0"],
               ["z0/%d" % b])
        act(T.eh[:, 320:640], T.eh[:, 0:320], AF.Copy, ["eh/0"], ["eh/1"])
        act(T.eh[:, 640:960], T.eh[:, 0:320], AF.Copy, ["eh/0"], ["eh/2"])
        quant("qzo", 0, 128, "z0", 0, ["z0"])
        for b in range(4):
            mm(b, 128, "wq", 128 * b, "qzo", 0)
        for b in range(4):
            act(T.h0[:, b:320:4], T["p%d" % b][:, 0:80], AF.Copy, ["p%d" % b], ["h0/%d" % b], scale=0.03125)
        for b in range(4):
            mm(4 + b, 240, "qun", 128 * b, came, 0)
        for b in range(4):
            tt(T.z1[:, b:960:4], T["p%d" % (4 + b)][:, 0:240], T.eh[:, b:960:4], OP.add, ["p%d" % (4 + b), "eh"],
               ["z1/%d" % b])
        quant("qz1", 0, 240, "z1", 0, ["z1"])
        for b in range(4):
            mm(b, 240, "wq", 128 * b, "qz1", 0)
        for b in range(4):
            o, i = T.h1[:, b:960:4], T["p%d" % b][:, 0:240]
            if b % 2:
                ts(o, i, 0.03125, None, OP.mult, None, ["p%d" % b], ["h1/%d" % b])
            else:
                act(o, i, AF.Copy, ["p%d" % b], ["h1/%d" % b], scale=0.03125)
        quant("qh", 0, 240, "h1", 0, ["h1"])
        send("qh", back, -1)
        quant("qho", 0, 128, "h0", 0, ["h0"])
        for b in range(4):
            mm(4 + b, 128, "qun", 128 * b, "qho", 0)
        if r == 0:
            second_flight_constants()
        ts(sm[:, 80:84], T.tab[:, 4:8], -16.0 * UNIT, None, OP.add, None, tabs, ["sm/la"])
        ts(sm[:, 84:88], T.tab[:, 0:4], 80.0 * UNIT, None, OP.add, None, tabs, ["sm/lb"])
        cp(T.tab[:, 8:12], T.tab[:, 0:4], tabs, ["tab/g"])
        tt(T.tab[:, 12:16], sm[:, 80:84], sm[:, 84:88], OP.min, ["sm/la", "sm/lb"], ["tab/l"])
        for k in range(4):
            ts(T.rks[:, 20 * k:20 * k + 20], T.rk[:], -15.875, UNIT, OP.add, OP.mult, ["rk"], ["rks/%d" % k])
        cp(T.tf[:], T.tab[:, 8:16].indirect(T.l80[:, 0:10]), ["tab/g", "tab/l", "l80"], ["tf"])
        s1, s2 = T.sl1, T.sl2
        tt(s1[:, 0:80], T.rks[:], T.tf[:, 80:160], OP.is_lt, ["rks", "tf"], ["sl1/a"])
        tt(s1[:, 80:160], T.rks[:], T.tf[:, 0:80], OP.is_ge, ["rks", "tf"], ["sl1/b"])
        tt(s1[:, 160:240], T.rks[:], T.tf[:, 0:80], OP.subtract, ["rks", "tf"], ["sl1/c"])
        tt(s1[:, 240:320], s1[:, 0:80], s1[:, 80:160], OP.mult, ["sl1/a", "sl1/b"], ["sl1/d"])
        ts(s1[:, 320:400], s1[:, 160:240], 1.0 / UNIT, None, OP.mult, None, ["sl1/c"], ["sl1/e"])
        tt(T.pl[:], s1[:, 320:400], T.kc[:], OP.add, ["sl1/e", "kc"], ["pl"])
        tt(s1[:, 0:80], T.pl[:], s1[:, 240:320], OP.mult, ["pl", "sl1/d"], ["sl1/a"])
        tt(s2[:, 0:40], s1[:, 0:40], s1[:, 40:80], OP.add, ["sl1/a"], ["sl2/a"])
        tt(s2[:, 40:60], s2[:, 0:20], s2[:, 20:40], OP.add, ["sl2/a"], ["sl2/b"])
        ts(s2[:, 60:80], s2[:, 40:60], 320.0, None, OP.add, None, ["sl2/b"], ["sl2/c"])
        cp(T.po[:], s2[:, 60:80], ["sl2/c"], ["po"])
        for t in range(4):
            ts(T.po16[:, 20 * t:20 * t + 20], T.po[:], 4.0, float(t), OP.mult, OP.add, ["po"], ["po16/%d" % t])
        for b in range(4):
            o, i = T.bk[:, 960 + b:1280:4], T["p%d" % (4 + b)][:, 0:80]
            act(o, i, AF.Copy, ["p%d" % (4 + b)], ["bk/own%d" % b], scale=2.0)
        if r == NR - 1:
            ts(T.rc[:, 0:240], T.ij[:, 0:240], 80.0, None, OP.add, None, ["ij"], ["rc/a"])
            ts(T.rc[:, 240:320], T.ij[:, 240:320], -240.0, None, OP.add, None, ["ij"], ["rc/b"])
            fill(T.rc[:, 320:336], -1.0, ["rc/c"])
            cp(T.po16[:, 80:100], T.po[:], ["po"], ["po16/s"])
            act(T.eq[:], T.rc[:, 0:336].indirect(T.po16[:, 80:100]), AF.Copy, ["rc", "po16/s"], ["eq"])
            for q in range(8):
                dma("S", lambda e, q=q: e.dma_start(T.sl[q:q + 1, :], T.eq[16 * q:16 * q + 1, :]), ("out", 0),
                    ["eq"], [])
            quant("qv", 0, 128, "vt", 0, ["vt"])
        for b in range(4):
            mm(b, 240, "qun", 128 * b, back, 0)
        for b in range(4):
            o, i = T.bk[:, b:960:4], T["p%d" % b][:, 0:240]
            if b % 2:
                ts(o, i, 2.0, None, OP.mult, None, ["p%d" % b], ["bk/%d" % b])
            else:
                act(o, i, AF.Copy, ["p%d" % b], ["bk/%d" % b], scale=2.0)
        for t in range(4):
            tt(xn[:, t:1280:4], T.bk[:, 0:1296].indirect(T.po16[:, 20 * t:20 * t + 20]), xa[:, t:1280:4], OP.add,
               ["bk", "po16/%d" % t, X], [XN + "/x%d" % t])

    X = "x%d" % NR
    quant("qx", 0, 320, X, 0, [X + "/x%d" % t for t in range(4)])
    mm(4, 320, "qv", 0, "qx", 0)
    dma("S", lambda e: e.dma_start(T.oc[:], T.qx[:].bitcast(dt.uint8)), ("out", 0), ["qx"], [])
    for k in range(4):
        dma("S", lambda e, k=k: e.dma_start(T.osc[4 * k:4 * k + 4, :], T.qxs[32 * k:32 * k + 4, :]), ("out", 0),
            ["qxs"], [])
    act(T.d1[:], T.p4[:, 0:320], AF.Copy, ["p4"], ["d1"])
    dma("A", lambda e: e.dma_start(T.y[:], T.d1[:]), ("out", 0), ["d1"], [])
    g.wait_ge(T.sem.out, 16 * (8 + 1 + 4 + 1))
    for n in sorted(lsn):
        g.wait_ge(T.sem["l" + n], lsn[n])
